import numpy as np
import ml_dtypes


def mxq(x, axis, fmt="e4m3"):
    dtype, down = {"e4m3": (ml_dtypes.float8_e4m3fn, 7), "e5m2": (ml_dtypes.float8_e5m2, 14)}[fmt]
    v = np.moveaxis(np.asarray(x, np.float32).astype(ml_dtypes.bfloat16).astype(np.float64), axis, -1)
    blocks = v.reshape(v.shape[:-1] + (-1, 32))
    amax = np.abs(blocks).max(-1, keepdims=True)
    byte = np.maximum(np.where(amax > 0, np.frexp(amax)[1] - 1 + 127, 0) - down, 1)
    scale = np.exp2(byte - 127.0)
    codes = (blocks / scale).astype(np.float32).astype(dtype).astype(np.float64)
    return np.moveaxis((codes * scale).reshape(v.shape), -1, axis)


WIDE = False


def mx_kscale(k):
    if not WIDE:
        return np.ones(k)
    levels = np.array([24, -24, 12, -12, 0])
    if k % 512:
        return np.exp2(np.random.permutation(np.resize(levels, k // 32))).repeat(32)
    a = np.empty((k // 512, 16))
    for p in range(k // 512):
        a[p, :8] = np.random.permutation(np.resize(levels, 8))
        for g in range(8):
            far = levels[np.abs(levels - a[p, g]) >= 10]
            a[p, g + 8] = far[np.random.randint(len(far))]
    return np.exp2(a.ravel()).repeat(32)


def f64(x):
    return np.asarray(x).astype(np.float64)


def striped(idx):
    return np.tile(idx.reshape(-1, 16).T, (8, 1)).astype(np.uint16)


def unstriped(offs):
    return offs[:16].T.reshape(-1).astype(np.int64)


E2M1 = np.array([0.0, 0.5, 1.0, 1.5, 2.0, 3.0, 4.0, 6.0, -0.0, -0.5, -1.0, -1.5, -2.0, -3.0, -4.0, -6.0])


def pack_weight(w, fmt):
    k, n = w.shape
    w = f64(np.asarray(w, np.float32).astype(ml_dtypes.bfloat16)).reshape(k // 32, 32, n)
    amax = np.abs(w).max(1)
    if fmt == "e4m3":
        byte = np.frexp(amax)[1] - 1 + 127 - 7
    else:
        mant, ex = np.frexp(amax / 6.0)
        byte = np.where(mant > 0.5, ex, ex - 1) + 127
    byte = np.clip(np.where(amax > 0, byte, 1), 1, 254)
    scaled = (w * np.exp2(127.0 - byte)[:, None, :]).reshape(k, n).astype(np.float32)
    by_word = np.ascontiguousarray(scaled.reshape(k // 512, 128, 4, n).transpose(0, 1, 3, 2))
    if fmt == "e4m3":
        words = by_word.astype(ml_dtypes.float8_e4m3fn).view(np.uint8)
    else:
        c = by_word.astype(ml_dtypes.float4_e2m1fn).view(np.uint8) & 0xF
        words = (c[..., 0::2] | (c[..., 1::2] << 4)).reshape(k // 512, 128, 2 * n)
    return np.ascontiguousarray(words), np.ascontiguousarray(byte.astype(np.uint8).reshape(k // 512, 16, n))


def unpack_weight(words, scales, fmt):
    g, _, n = scales.shape
    words = np.ascontiguousarray(words).reshape(g, 128, n, -1)
    if fmt == "e4m3":
        vals = words.view(ml_dtypes.float8_e4m3fn).astype(np.float64)
    else:
        nib = np.empty((g, 128, n, 4), np.uint8)
        nib[..., 0::2] = words & 0xF
        nib[..., 1::2] = words >> 4
        vals = E2M1[nib]
    vals = vals * np.repeat(np.exp2(scales.astype(np.float64) - 127.0), 8, axis=1)[..., None]
    return vals.transpose(0, 1, 3, 2).reshape(g * 512, n)


def pack_table4(v):
    words, scales = pack_weight(v, "e2m1")
    g, t = words.shape[0] // 2, v.shape[1]
    return np.ascontiguousarray(words.reshape(g, 2, 128, t, 2).transpose(0, 2, 3, 1, 4).reshape(g, 128, t, 4)), scales


def unpack_table4(words, scales):
    g, _, t, _ = words.shape
    return unpack_weight(words.reshape(g, 128, t, 2, 2).transpose(0, 3, 1, 2, 4).reshape(2 * g, 128, 2 * t), scales, "e2m1")


def planes(y):
    n, m = y.shape
    v = y.astype(np.float32).astype(ml_dtypes.bfloat16).astype(np.float64).reshape(n // 32, 32, m)
    top = np.abs(v).max(1)
    byte = np.clip(np.where(top > 0, np.frexp(top)[1] - 1 + 127 - 7, 1), 1, 254)
    codes = (v * np.exp2(127.0 - byte)[:, None, :]).reshape(n, m).astype(np.float32).astype(ml_dtypes.float8_e4m3fn).view(np.uint8)
    words = codes.reshape(n // 512, 128, 4, m).transpose(0, 1, 3, 2)
    return np.ascontiguousarray(words), np.ascontiguousarray(byte.astype(np.uint8).reshape(n // 512, 16, m))


K, R, N, T, J = 1024, 512, 512, 4096, 1024


def setup_inputs():
    n = np.random.standard_normal
    s = mx_kscale(K)[:, None]
    u = mx_kscale(R)[:, None]
    p_tab = pack_table4(n((K, T)) * s)
    p_wb = pack_weight(0.7 * n((K, N)) / np.sqrt(K) / s, "e4m3")
    p_upw = pack_weight(2.0 * n((R, N)) / np.sqrt(R) / u, "e2m1")
    return {
        "tab_words": p_tab[0],
        "tab_scales": p_tab[1],
        "wb_words": p_wb[0],
        "wb_scales": p_wb[1],
        "dn": (n((K, R)) / np.sqrt(K) / s * u.T).astype(np.float32),
        "upw_words": p_upw[0],
        "upw_scales": p_upw[1],
        "x0T": (n((N, T))).astype(np.float32),
        "b": (0.3 * n(N)).astype(np.float32),
        "offs": striped(np.random.permutation(T)[:J]),
    }


def reference(tab_words, tab_scales, wb_words, wb_scales, dn, upw_words, upw_scales, x0T, b, offs):
    idx = unstriped(offs)
    tab_ = unpack_table4(tab_words, tab_scales)[:, idx]
    wb_ = unpack_weight(wb_words, wb_scales, "e4m3")
    dn_ = mxq(f64(dn), 0, "e4m3")
    hs = dn_.T @ tab_
    h = np.maximum(hs, 0.0)
    h_ = mxq(h, 0, "e4m3")
    upw_ = unpack_weight(upw_words, upw_scales, "e2m1")
    y = wb_.T @ tab_ + upw_.T @ h_
    out_0 = f64(x0T)[:, idx] * (y + f64(b)[:, None]) + f64(x0T)[:, idx]
    return (out_0,) + planes(out_0)

@@ -1,0 +1,238 @@
+from contextlib import ExitStack
+
+import concourse.mybir as mybir
+
+K, R, N, T, J = 1024, 512, 512, 4096, 1024
+FLOPS = 2 * J * (K * R + K * N + R * N)
+
+F32 = mybir.dt.float32
+BF16 = mybir.dt.bfloat16
+I32 = mybir.dt.int32
+U32 = mybir.dt.uint32
+U16 = mybir.dt.uint16
+U8 = mybir.dt.uint8
+FP8X4 = mybir.dt.float8_e4m3fn_x4
+FP4X4 = mybir.dt.float4_e2m1fn_x4
+ACT = mybir.ActivationFunctionType
+ALU = mybir.AluOpType
+
+P = 128
+PACK = 4
+PASSES = K // (P * PACK)
+HALF = 512
+CHUNK = 128
+PIECE = 256
+LIST_ROWS = 16
+
+
+def tile_list_xcross_reluP_kernel(
+    tc, tab_words, tab_scales, wb_words, wb_scales, dn, upw_words, upw_scales, x0T, b, offs, out_0, out_1, out_2
+):
+    nc = tc.nc
+    halves = J // HALF
+    pieces = J // PIECE
+
+    with ExitStack() as ctx:
+        keep = ctx.enter_context(tc.tile_pool(name="keep", bufs=1))
+        psum = ctx.enter_context(tc.psum_pool(name="psum", bufs=1))
+
+        def sb(shape, dtype, name, tag=None):
+            return keep.tile(shape, dtype, name=name, tag=tag or name, align_bytes=64)
+
+        def listed(window, j0, j1):
+            return window.indirect(offsets[:, j0 // LIST_ROWS : j1 // LIST_ROWS])
+
+        offsets = keep.tile([P, J // LIST_ROWS], U16, name="offsets")
+        nc.sync.dma_start(offsets[:], offs)
+
+        tab_sc = sb([P, T], U8, "tab_sc")
+        nc.vector.memset(tab_sc[:, 0 : T // 2].bitcast(I32), 0)
+        nc.gpsimd.memset(tab_sc[:, T // 2 : T].bitcast(I32), 0)
+        sc_rows = tab_scales.rearrange("a (q r) t -> r q a t", r=PACK)
+        for r in range(PACK):
+            nc.scalar.dma_start(tab_sc[r:P:16, :].bitcast(I32), sc_rows[r].bitcast(I32))
+
+        tab_w = sb([P, T], U32, "tab_w")
+        nc.sync.dma_start(tab_w[:].bitcast(I32), tab_words[0].rearrange("p t i -> p (t i)").bitcast(I32))
+        dn_raw = []
+        for a in range(PASSES):
+            raw = sb([P, PACK, R], F32, "dn_raw%d" % a)
+            nc.sync.dma_start(raw[:], dn[512 * a : 512 * (a + 1), :].rearrange("(p i) r -> p i r", i=PACK))
+            dn_raw.append(raw)
+
+        b_col = sb([P, PACK], F32, "b_col")
+        nc.scalar.dma_start(b_col[:], b.rearrange("(p t) -> p t", t=PACK))
+        w_sc_raw = sb([P, PASSES + 1, N], U8, "w_sc_raw")
+        nc.gpsimd.memset(w_sc_raw[:].bitcast(I32), 0)
+        for q in range(4):
+            nc.scalar.dma_start(
+                w_sc_raw[32 * q : 32 * q + 4, 0:PASSES, :].bitcast(I32),
+                wb_scales[:, 4 * q : 4 * q + 4, :].rearrange("a r n -> r a n").bitcast(I32),
+            )
+            nc.scalar.dma_start(
+                w_sc_raw[32 * q : 32 * q + 4, PASSES, :].bitcast(I32), upw_scales[0, 4 * q : 4 * q + 4, :].bitcast(I32)
+            )
+
+        b_one = sb([P, PACK], F32, "b_one")
+        nc.scalar.activation(b_one[:], b_col[:], ACT.Copy, bias=1.0)
+
+        g_sc1 = sb([P, J], U8, "g_sc1")
+        nc.vector.memset(g_sc1[:].bitcast(I32), 0)
+        g_sc0 = sb([P, J], U8, "g_sc0")
+        nc.vector.tensor_copy(g_sc0[:], listed(tab_sc[:], 0, J))
+        nc.sync.dma_start(g_sc1[0 : P - 16, :].bitcast(I32), g_sc0[16:P, :].bitcast(I32))
+        g_sc = [g_sc0, g_sc1]
+
+        wb_raw = sb([P, PASSES, N], U32, "wb_raw")
+        nc.sync.dma_start(wb_raw[:].bitcast(I32), wb_words.rearrange("a p n i -> p a (n i)").bitcast(I32))
+        up_raw = sb([P, 2 * N], U8, "up_raw")
+        nc.sync.dma_start(up_raw[:].bitcast(I32), upw_words[0].bitcast(I32))
+
+        v_w = []
+        for h in range(halves):
+            both = sb([P, HALF], U32, "both%d" % h)
+            nc.vector.tensor_copy(both[:], listed(tab_w[:], h * HALF, (h + 1) * HALF))
+            parted = sb([P, PASSES, 2 * HALF], U8, "parted%d" % h)
+            nc.vector.tensor_copy(
+                parted[:].bitcast(U16), both[:].bitcast(U16).rearrange("p (j a) -> p a j", a=PASSES)
+            )
+            v_w.append(parted)
+
+        dn_w, dn_sc = [], []
+        for a in range(PASSES):
+            grouped = sb([P, PACK * R], BF16, "dn_grouped%d" % a)
+            dst = grouped[:].rearrange("p (t m i) -> p t m i", t=PACK, i=PACK)
+            src = dn_raw[a][:].rearrange("p i (m t) -> p t m i", t=PACK)
+            if a == 0:
+                nc.scalar.copy(dst, src)
+            else:
+                nc.vector.tensor_copy(dst, src)
+            codes = sb([P, R], U32, "dn_w%d" % a)
+            scales = sb([P, R], U8, "dn_sc%d" % a)
+            nc.vector.quantize_mx(out=codes[:].bitcast(FP8X4), scales=scales[:], in_=grouped[:])
+            dn_w.append(codes)
+            dn_sc.append(scales)
+
+        wb = sb([P, PASSES, N], U32, "wb")
+        nc.vector.tensor_copy(
+            wb[:].bitcast(I32).rearrange("p a (t m) -> p a t m", t=PACK),
+            wb_raw[:].bitcast(I32).rearrange("p a (m t) -> p a t m", t=PACK),
+        )
+        up = sb([P, 2 * N], U8, "up")
+        nc.vector.tensor_copy(
+            up[:].bitcast(U16).rearrange("p (t m) -> p t m", t=PACK),
+            up_raw[:].bitcast(U16).rearrange("p (m t) -> p t m", t=PACK),
+        )
+
+        w_sc = sb([P, PASSES + 1, N], U8, "w_sc")
+        nc.vector.tensor_copy(
+            w_sc[:].rearrange("p a (t m) -> p a t m", t=PACK), w_sc_raw[:].rearrange("p a (m t) -> p a t m", t=PACK)
+        )
+
+        x_rows = x0T.rearrange("(p t) c -> t p c", t=PACK)
+        x_win = []
+        for t in range(PACK):
+            win = sb([P, T], F32, "x_win%d" % t)
+            nc.sync.dma_start(win[:], x_rows[t])
+            x_win.append(win)
+
+        h_w, h_sc = [], []
+        for h in range(halves):
+            h_bf = sb([P, HALF * PACK], BF16, "h_bf%d" % h)
+            for c in range(HALF // CHUNK):
+                bank = psum.tile([P, PACK, CHUNK], F32, name="hs%d_%d" % (h, c), tag="bank%d" % (4 + c))
+                j0 = h * HALF + c * CHUNK
+                for t in range(PACK):
+                    for a in range(PASSES):
+                        nc.tensor.matmul_mx(
+                            out=bank[:, t, :],
+                            lhsT=dn_w[a][:, t * P : (t + 1) * P].bitcast(FP8X4),
+                            lhsT_scale=dn_sc[a][:, t * P : (t + 1) * P],
+                            rhs=v_w[h][:, a, 2 * c * CHUNK : 2 * (c + 1) * CHUNK].bitcast(FP4X4),
+                            rhs_scale=g_sc[a][:, j0 : j0 + CHUNK],
+                            start=(a == 0),
+                            stop=(a == PASSES - 1),
+                        )
+                nc.scalar.activation(
+                    h_bf[:, c * CHUNK * PACK : (c + 1) * CHUNK * PACK].rearrange("p (j t) -> p j t", t=PACK),
+                    bank[:].rearrange("p t j -> p j t"),
+                    ACT.Relu,
+                )
+            codes = sb([P, HALF], U32, "h_w%d" % h)
+            scales = sb([P, HALF], U8, "h_sc%d" % h)
+            nc.vector.quantize_mx(out=codes[:].bitcast(FP8X4), scales=scales[:], in_=h_bf[:])
+            h_w.append(codes)
+            h_sc.append(scales)
+
+        x_g = []
+        for t in range(2):
+            picked = sb([P, J], F32, "x_g%d" % t)
+            nc.vector.tensor_copy(picked[:], listed(x_win[t][:], 0, J))
+            x_g.append(picked)
+
+        o_lo = sb([P, 2, J], F32, "o_lo")
+        z = [sb([P, J], F32, "z%d" % t) for t in (2, 3)]
+        for h in range(halves):
+            cols = slice(h * HALF, (h + 1) * HALF)
+            for t in range(PACK):
+                bank = psum.tile([P, HALF], F32, name="y%d_%d" % (h, t), tag="bank%d" % (4 * h + t))
+                rows = slice(t * P, (t + 1) * P)
+                for a in range(PASSES):
+                    nc.tensor.matmul_mx(
+                        out=bank[:],
+                        lhsT=wb[:, a, rows].bitcast(FP8X4),
+                        lhsT_scale=w_sc[:, a, rows],
+                        rhs=v_w[h][:, a, :].bitcast(FP4X4),
+                        rhs_scale=g_sc[a][:, cols],
+                        start=(a == 0),
+                        stop=False,
+                    )
+                nc.tensor.matmul_mx(
+                    out=bank[:],
+                    lhsT=up[:, 2 * t * P : 2 * (t + 1) * P].bitcast(FP4X4),
+                    lhsT_scale=w_sc[:, PASSES, rows],
+                    rhs=h_w[h][:].bitcast(FP8X4),
+                    rhs_scale=h_sc[h][:],
+                    start=False,
+                    stop=True,
+                )
+                if t < 2:
+                    nc.vector.scalar_tensor_tensor(
+                        o_lo[:, t, cols], bank[:], b_one[:, t : t + 1], x_g[t][:, cols], ALU.add, ALU.mult
+                    )
+                else:
+                    nc.scalar.activation(z[t - 2][:, cols], bank[:], ACT.Identity, bias=b_one[:, t : t + 1])
+
+        out_rows = out_0.rearrange("(p t) j -> p t j", t=PACK)
+        nc.sync.dma_start(out_rows[:, 0:2, :], o_lo[:])
+
+        o_bf = [sb([P, PIECE, PACK], BF16, "o_bf%d" % c) for c in range(pieces)]
+        o_hi = [sb([P, 2, PIECE], F32, "o_hi%d" % c) for c in range(pieces)]
+        for c in range(pieces):
+            cols = slice(c * PIECE, (c + 1) * PIECE)
+            nc.scalar.copy(o_bf[c][:, :, 0:2], o_lo[:, :, cols].rearrange("p t j -> p j t"))
+        for c in range(pieces):
+            cols = slice(c * PIECE, (c + 1) * PIECE)
+            nc.vector.tensor_tensor(o_hi[c][:, 0, :], listed(x_win[2][:], cols.start, cols.stop), z[0][:, cols], ALU.mult)
+
+        o_sc = sb([P, J], U8, "o_sc")
+        words_out = out_1[0].rearrange("p j i -> p (j i)").bitcast(I32)
+        o_w = [sb([P, PIECE], U32, "o_w%d" % c) for c in range(pieces)]
+
+        def finish(c):
+            cols = slice(c * PIECE, (c + 1) * PIECE)
+            nc.vector.quantize_mx(
+                out=o_w[c][:].bitcast(FP8X4), scales=o_sc[:, cols], in_=o_bf[c][:].rearrange("p j t -> p (j t)")
+            )
+            nc.sync.dma_start(words_out[:, cols], o_w[c][:].bitcast(I32))
+
+        for c in range(pieces):
+            cols = slice(c * PIECE, (c + 1) * PIECE)
+            nc.vector.tensor_tensor(o_hi[c][:, 1, :], listed(x_win[3][:], cols.start, cols.stop), z[1][:, cols], ALU.mult)
+            nc.sync.dma_start(out_rows[:, 2:4, cols], o_hi[c][:])
+            nc.scalar.copy(o_bf[c][:, :, 2:4], o_hi[c][:].rearrange("p t j -> p j t"))
+            if c > 0:
+                finish(c - 1)
+        finish(pieces - 1)
+        for q in range(4):
+            nc.sync.dma_start(out_2[0, 4 * q : 4 * q + 4, :].bitcast(I32), o_sc[32 * q : 32 * q + 4, :].bitcast(I32))

@@ -45,36 +45,21 @@ def tile_list_xcross_reluP_kernel(
         offsets = keep.tile([P, J // LIST_ROWS], U16, name="offsets")
         nc.sync.dma_start(offsets[:], offs)
 
+        def load_dn(a):
+            raw = sb([P, PACK, R], F32, "dn_raw%d" % a)
+            nc.sync.dma_start(raw[:], dn[512 * a : 512 * (a + 1), :].rearrange("(p i) r -> p i r", i=PACK))
+            return raw
+
         tab_sc = sb([P, T], U8, "tab_sc")
         nc.vector.memset(tab_sc[:, 0 : T // 2].bitcast(I32), 0)
         nc.gpsimd.memset(tab_sc[:, T // 2 : T].bitcast(I32), 0)
+        dn_raw = [load_dn(0)]
         sc_rows = tab_scales.rearrange("a (q r) t -> r q a t", r=PACK)
         for r in range(PACK):
-            nc.scalar.dma_start(tab_sc[r:P:16, :].bitcast(I32), sc_rows[r].bitcast(I32))
-
+            nc.sync.dma_start(tab_sc[r:P:16, :].bitcast(I32), sc_rows[r].bitcast(I32))
+        dn_raw.append(load_dn(1))
         tab_w = sb([P, T], U32, "tab_w")
         nc.sync.dma_start(tab_w[:].bitcast(I32), tab_words[0].rearrange("p t i -> p (t i)").bitcast(I32))
-        dn_raw = []
-        for a in range(PASSES):
-            raw = sb([P, PACK, R], F32, "dn_raw%d" % a)
-            nc.sync.dma_start(raw[:], dn[512 * a : 512 * (a + 1), :].rearrange("(p i) r -> p i r", i=PACK))
-            dn_raw.append(raw)
-
-        b_col = sb([P, PACK], F32, "b_col")
-        nc.scalar.dma_start(b_col[:], b.rearrange("(p t) -> p t", t=PACK))
-        w_sc_raw = sb([P, PASSES + 1, N], U8, "w_sc_raw")
-        nc.gpsimd.memset(w_sc_raw[:].bitcast(I32), 0)
-        for q in range(4):
-            nc.scalar.dma_start(
-                w_sc_raw[32 * q : 32 * q + 4, 0:PASSES, :].bitcast(I32),
-                wb_scales[:, 4 * q : 4 * q + 4, :].rearrange("a r n -> r a n").bitcast(I32),
-            )
-            nc.scalar.dma_start(
-                w_sc_raw[32 * q : 32 * q + 4, PASSES, :].bitcast(I32), upw_scales[0, 4 * q : 4 * q + 4, :].bitcast(I32)
-            )
-
-        b_one = sb([P, PACK], F32, "b_one")
-        nc.scalar.activation(b_one[:], b_col[:], ACT.Copy, bias=1.0)
 
         g_sc1 = sb([P, J], U8, "g_sc1")
         nc.vector.memset(g_sc1[:].bitcast(I32), 0)
@@ -88,6 +73,37 @@ def tile_list_xcross_reluP_kernel(
         up_raw = sb([P, 2 * N], U8, "up_raw")
         nc.sync.dma_start(up_raw[:].bitcast(I32), upw_words[0].bitcast(I32))
 
+        b_col = sb([P, PACK], F32, "b_col")
+        nc.gpsimd.dma_start(b_col[:], b.rearrange("(p t) -> p t", t=PACK))
+        b_one = sb([P, PACK], F32, "b_one")
+        nc.gpsimd.tensor_scalar(b_one[:], b_col[:], 1.0, None, ALU.add)
+
+        wb_sc_raw = sb([P, PASSES, N], U8, "wb_sc_raw")
+        nc.vector.memset(wb_sc_raw[:].bitcast(I32), 0)
+        up_sc_raw = sb([P, N], U8, "up_sc_raw")
+        nc.gpsimd.memset(up_sc_raw[:].bitcast(I32), 0)
+        for q in range(4):
+            nc.sync.dma_start(
+                wb_sc_raw[32 * q : 32 * q + 4, :, :].bitcast(I32),
+                wb_scales[:, 4 * q : 4 * q + 4, :].rearrange("a r n -> r a n").bitcast(I32),
+            )
+            nc.gpsimd.dma_start(
+                up_sc_raw[32 * q : 32 * q + 4, :].bitcast(I32), upw_scales[0, 4 * q : 4 * q + 4, :].bitcast(I32)
+            )
+
+        dn_w, dn_sc = [], []
+        for a in range(PASSES):
+            grouped = sb([P, PACK * R], BF16, "dn_grouped%d" % a)
+            nc.scalar.copy(
+                grouped[:].rearrange("p (t m i) -> p m i t", t=PACK, i=PACK),
+                dn_raw[a][:].rearrange("p i (m t) -> p m i t", t=PACK),
+            )
+            codes = sb([P, R], U32, "dn_w%d" % a)
+            scales = sb([P, R], U8, "dn_sc%d" % a)
+            nc.vector.quantize_mx(out=codes[:].bitcast(FP8X4), scales=scales[:], in_=grouped[:])
+            dn_w.append(codes)
+            dn_sc.append(scales)
+
         v_w = []
         for h in range(halves):
             both = sb([P, HALF], U32, "both%d" % h)
@@ -98,35 +114,23 @@ def tile_list_xcross_reluP_kernel(
             )
             v_w.append(parted)
 
-        dn_w, dn_sc = [], []
-        for a in range(PASSES):
-            grouped = sb([P, PACK * R], BF16, "dn_grouped%d" % a)
-            dst = grouped[:].rearrange("p (t m i) -> p t m i", t=PACK, i=PACK)
-            src = dn_raw[a][:].rearrange("p i (m t) -> p t m i", t=PACK)
-            if a == 0:
-                nc.scalar.copy(dst, src)
-            else:
-                nc.vector.tensor_copy(dst, src)
-            codes = sb([P, R], U32, "dn_w%d" % a)
-            scales = sb([P, R], U8, "dn_sc%d" % a)
-            nc.vector.quantize_mx(out=codes[:].bitcast(FP8X4), scales=scales[:], in_=grouped[:])
-            dn_w.append(codes)
-            dn_sc.append(scales)
-
         wb = sb([P, PASSES, N], U32, "wb")
         nc.vector.tensor_copy(
-            wb[:].bitcast(I32).rearrange("p a (t m) -> p a t m", t=PACK),
-            wb_raw[:].bitcast(I32).rearrange("p a (m t) -> p a t m", t=PACK),
+            wb[:].bitcast(I32).rearrange("p a (t m) -> p a m t", t=PACK),
+            wb_raw[:].bitcast(I32).rearrange("p a (m t) -> p a m t", t=PACK),
         )
         up = sb([P, 2 * N], U8, "up")
         nc.vector.tensor_copy(
-            up[:].bitcast(U16).rearrange("p (t m) -> p t m", t=PACK),
-            up_raw[:].bitcast(U16).rearrange("p (m t) -> p t m", t=PACK),
+            up[:].bitcast(U16).rearrange("p (t m) -> p m t", t=PACK),
+            up_raw[:].bitcast(U16).rearrange("p (m t) -> p m t", t=PACK),
         )
-
-        w_sc = sb([P, PASSES + 1, N], U8, "w_sc")
+        wb_sc = sb([P, PASSES, N], U8, "wb_sc")
         nc.vector.tensor_copy(
-            w_sc[:].rearrange("p a (t m) -> p a t m", t=PACK), w_sc_raw[:].rearrange("p a (m t) -> p a t m", t=PACK)
+            wb_sc[:].rearrange("p a (t m) -> p a m t", t=PACK), wb_sc_raw[:].rearrange("p a (m t) -> p a m t", t=PACK)
+        )
+        up_sc = sb([P, N], U8, "up_sc", tag="both1")
+        nc.vector.tensor_copy(
+            up_sc[:].rearrange("p (t m) -> p m t", t=PACK), up_sc_raw[:].rearrange("p (m t) -> p m t", t=PACK)
         )
 
         x_rows = x0T.rearrange("(p t) c -> t p c", t=PACK)
@@ -181,7 +185,7 @@ def tile_list_xcross_reluP_kernel(
                     nc.tensor.matmul_mx(
                         out=bank[:],
                         lhsT=wb[:, a, rows].bitcast(FP8X4),
-                        lhsT_scale=w_sc[:, a, rows],
+                        lhsT_scale=wb_sc[:, a, rows],
                         rhs=v_w[h][:, a, :].bitcast(FP4X4),
                         rhs_scale=g_sc[a][:, cols],
                         start=(a == 0),
@@ -190,7 +194,7 @@ def tile_list_xcross_reluP_kernel(
                 nc.tensor.matmul_mx(
                     out=bank[:],
                     lhsT=up[:, 2 * t * P : 2 * (t + 1) * P].bitcast(FP4X4),
-                    lhsT_scale=w_sc[:, PASSES, rows],
+                    lhsT_scale=up_sc[:, rows],
                     rhs=h_w[h][:].bitcast(FP8X4),
                     rhs_scale=h_sc[h][:],
                     start=False,

@@ -57,21 +57,12 @@ def tile_list_xcross_reluP_kernel(
         sc_rows = tab_scales.rearrange("a (q r) t -> r q a t", r=PACK)
         for r in range(PACK):
             nc.sync.dma_start(tab_sc[r:P:16, :].bitcast(I32), sc_rows[r].bitcast(I32))
-        dn_raw.append(load_dn(1))
         tab_w = sb([P, T], U32, "tab_w")
         nc.sync.dma_start(tab_w[:].bitcast(I32), tab_words[0].rearrange("p t i -> p (t i)").bitcast(I32))
-
-        g_sc1 = sb([P, J], U8, "g_sc1")
-        nc.vector.memset(g_sc1[:].bitcast(I32), 0)
-        g_sc0 = sb([P, J], U8, "g_sc0")
-        nc.vector.tensor_copy(g_sc0[:], listed(tab_sc[:], 0, J))
-        nc.sync.dma_start(g_sc1[0 : P - 16, :].bitcast(I32), g_sc0[16:P, :].bitcast(I32))
-        g_sc = [g_sc0, g_sc1]
+        dn_raw.append(load_dn(1))
 
         wb_raw = sb([P, PASSES, N], U32, "wb_raw")
         nc.sync.dma_start(wb_raw[:].bitcast(I32), wb_words.rearrange("a p n i -> p a (n i)").bitcast(I32))
-        up_raw = sb([P, 2 * N], U8, "up_raw")
-        nc.sync.dma_start(up_raw[:].bitcast(I32), upw_words[0].bitcast(I32))
 
         b_col = sb([P, PACK], F32, "b_col")
         nc.gpsimd.dma_start(b_col[:], b.rearrange("(p t) -> p t", t=PACK))
@@ -91,6 +82,25 @@ def tile_list_xcross_reluP_kernel(
                 up_sc_raw[32 * q : 32 * q + 4, :].bitcast(I32), upw_scales[0, 4 * q : 4 * q + 4, :].bitcast(I32)
             )
 
+        g_sc1 = sb([P, J], U8, "g_sc1")
+        nc.vector.memset(g_sc1[:].bitcast(I32), 0)
+        g_sc0 = sb([P, J], U8, "g_sc0")
+        nc.vector.tensor_copy(g_sc0[:], listed(tab_sc[:], 0, J))
+        nc.sync.dma_start(g_sc1[0 : P - 16, :].bitcast(I32), g_sc0[16:P, :].bitcast(I32))
+        g_sc = [g_sc0, g_sc1]
+
+        x_rows = x0T.rearrange("(p t) c -> t p c", t=PACK)
+
+        def load_x(t):
+            win = sb([P, T], F32, "x_win%d" % t)
+            nc.sync.dma_start(win[:], x_rows[t])
+            return win
+
+        x_win = [load_x(0)]
+        up_raw = sb([P, 2 * N], U8, "up_raw")
+        nc.sync.dma_start(up_raw[:].bitcast(I32), upw_words[0].bitcast(I32))
+        x_win.extend([load_x(t) for t in range(1, PACK)])
+
         dn_w, dn_sc = [], []
         for a in range(PASSES):
             grouped = sb([P, PACK * R], BF16, "dn_grouped%d" % a)
@@ -98,7 +108,7 @@ def tile_list_xcross_reluP_kernel(
                 grouped[:].rearrange("p (t m i) -> p m i t", t=PACK, i=PACK),
                 dn_raw[a][:].rearrange("p i (m t) -> p m i t", t=PACK),
             )
-            codes = sb([P, R], U32, "dn_w%d" % a)
+            codes = sb([P, R], U32, "dn_w%d" % a, tag=("tab_sc", "dn_w1")[a])
             scales = sb([P, R], U8, "dn_sc%d" % a)
             nc.vector.quantize_mx(out=codes[:].bitcast(FP8X4), scales=scales[:], in_=grouped[:])
             dn_w.append(codes)
@@ -133,13 +143,6 @@ def tile_list_xcross_reluP_kernel(
             up_sc[:].rearrange("p (t m) -> p m t", t=PACK), up_sc_raw[:].rearrange("p (m t) -> p m t", t=PACK)
         )
 
-        x_rows = x0T.rearrange("(p t) c -> t p c", t=PACK)
-        x_win = []
-        for t in range(PACK):
-            win = sb([P, T], F32, "x_win%d" % t)
-            nc.sync.dma_start(win[:], x_rows[t])
-            x_win.append(win)
-
         h_w, h_sc = [], []
         for h in range(halves):
             h_bf = sb([P, HALF * PACK], BF16, "h_bf%d" % h)
@@ -168,19 +171,12 @@ def tile_list_xcross_reluP_kernel(
             h_w.append(codes)
             h_sc.append(scales)
 
-        x_g = []
-        for t in range(2):
-            picked = sb([P, J], F32, "x_g%d" % t)
-            nc.vector.tensor_copy(picked[:], listed(x_win[t][:], 0, J))
-            x_g.append(picked)
-
-        o_lo = sb([P, 2, J], F32, "o_lo")
-        z = [sb([P, J], F32, "z%d" % t) for t in (2, 3)]
-        for h in range(halves):
-            cols = slice(h * HALF, (h + 1) * HALF)
-            for t in range(PACK):
-                bank = psum.tile([P, HALF], F32, name="y%d_%d" % (h, t), tag="bank%d" % (4 * h + t))
-                rows = slice(t * P, (t + 1) * P)
+        z = [sb([P, J], F32, "z%d" % t) for t in range(PACK)]
+        for t in range(PACK):
+            rows = slice(t * P, (t + 1) * P)
+            for h in range(halves):
+                cols = slice(h * HALF, (h + 1) * HALF)
+                bank = psum.tile([P, HALF], F32, name="y%d_%d" % (t, h), tag="bank%d" % (halves * t + h))
                 for a in range(PASSES):
                     nc.tensor.matmul_mx(
                         out=bank[:],
@@ -200,12 +196,13 @@ def tile_list_xcross_reluP_kernel(
                     start=False,
                     stop=True,
                 )
-                if t < 2:
-                    nc.vector.scalar_tensor_tensor(
-                        o_lo[:, t, cols], bank[:], b_one[:, t : t + 1], x_g[t][:, cols], ALU.add, ALU.mult
-                    )
-                else:
-                    nc.scalar.activation(z[t - 2][:, cols], bank[:], ACT.Identity, bias=b_one[:, t : t + 1])
+                nc.scalar.activation(z[t][:, cols], bank[:], ACT.Identity, bias=b_one[:, t : t + 1])
+
+        o_lo = sb([P, 2, J], F32, "o_lo")
+        for t in range(2):
+            for h in range(halves):
+                cols = slice(h * HALF, (h + 1) * HALF)
+                nc.vector.tensor_tensor(o_lo[:, t, cols], listed(x_win[t][:], cols.start, cols.stop), z[t][:, cols], ALU.mult)
 
         out_rows = out_0.rearrange("(p t) j -> p t j", t=PACK)
         nc.sync.dma_start(out_rows[:, 0:2, :], o_lo[:])
@@ -217,7 +214,7 @@ def tile_list_xcross_reluP_kernel(
             nc.scalar.copy(o_bf[c][:, :, 0:2], o_lo[:, :, cols].rearrange("p t j -> p j t"))
         for c in range(pieces):
             cols = slice(c * PIECE, (c + 1) * PIECE)
-            nc.vector.tensor_tensor(o_hi[c][:, 0, :], listed(x_win[2][:], cols.start, cols.stop), z[0][:, cols], ALU.mult)
+            nc.vector.tensor_tensor(o_hi[c][:, 0, :], listed(x_win[2][:], cols.start, cols.stop), z[2][:, cols], ALU.mult)
 
         o_sc = sb([P, J], U8, "o_sc")
         words_out = out_1[0].rearrange("p j i -> p (j i)").bitcast(I32)
@@ -232,11 +229,11 @@ def tile_list_xcross_reluP_kernel(
 
         for c in range(pieces):
             cols = slice(c * PIECE, (c + 1) * PIECE)
-            nc.vector.tensor_tensor(o_hi[c][:, 1, :], listed(x_win[3][:], cols.start, cols.stop), z[1][:, cols], ALU.mult)
+            nc.vector.tensor_tensor(o_hi[c][:, 1, :], listed(x_win[3][:], cols.start, cols.stop), z[3][:, cols], ALU.mult)
             nc.sync.dma_start(out_rows[:, 2:4, cols], o_hi[c][:])
             nc.scalar.copy(o_bf[c][:, :, 2:4], o_hi[c][:].rearrange("p t j -> p j t"))
             if c > 0:
                 finish(c - 1)
         finish(pieces - 1)
         for q in range(4):
-            nc.sync.dma_start(out_2[0, 4 * q : 4 * q + 4, :].bitcast(I32), o_sc[32 * q : 32 * q + 4, :].bitcast(I32))
+            nc.scalar.dma_start(out_2[0, 4 * q : 4 * q + 4, :].bitcast(I32), o_sc[32 * q : 32 * q + 4, :].bitcast(I32))

@@ -21,7 +21,8 @@ PACK = 4
 PASSES = K // (P * PACK)
 HALF = 512
 CHUNK = 128
-PIECE = 256
+EDGES = (0, 128, 384, 640, 896, 1024)
+STORE_CUT = 640
 LIST_ROWS = 16
 
 
@@ -30,7 +31,6 @@ def tile_list_xcross_reluP_kernel(
 ):
     nc = tc.nc
     halves = J // HALF
-    pieces = J // PIECE
 
     with ExitStack() as ctx:
         keep = ctx.enter_context(tc.tile_pool(name="keep", bufs=1))
@@ -45,49 +45,41 @@ def tile_list_xcross_reluP_kernel(
         offsets = keep.tile([P, J // LIST_ROWS], U16, name="offsets")
         nc.sync.dma_start(offsets[:], offs)
 
-        def load_dn(a):
-            raw = sb([P, PACK, R], F32, "dn_raw%d" % a)
-            nc.sync.dma_start(raw[:], dn[512 * a : 512 * (a + 1), :].rearrange("(p i) r -> p i r", i=PACK))
-            return raw
+        dn_rows = dn.rearrange("(a p i) r -> a p i r", a=PASSES, i=PACK)
+        dn_raw = [sb([P, PACK, R], F32, "dn_raw%d" % a) for a in range(PASSES)]
 
-        tab_sc = sb([P, T], U8, "tab_sc")
-        nc.vector.memset(tab_sc[:, 0 : T // 2].bitcast(I32), 0)
-        nc.gpsimd.memset(tab_sc[:, T // 2 : T].bitcast(I32), 0)
-        dn_raw = [load_dn(0)]
-        sc_rows = tab_scales.rearrange("a (q r) t -> r q a t", r=PACK)
-        for r in range(PACK):
-            nc.sync.dma_start(tab_sc[r:P:16, :].bitcast(I32), sc_rows[r].bitcast(I32))
-        tab_w = sb([P, T], U32, "tab_w")
-        nc.sync.dma_start(tab_w[:].bitcast(I32), tab_words[0].rearrange("p t i -> p (t i)").bitcast(I32))
-        dn_raw.append(load_dn(1))
-
-        wb_raw = sb([P, PASSES, N], U32, "wb_raw")
-        nc.sync.dma_start(wb_raw[:].bitcast(I32), wb_words.rearrange("a p n i -> p a (n i)").bitcast(I32))
-
-        b_col = sb([P, PACK], F32, "b_col")
-        nc.gpsimd.dma_start(b_col[:], b.rearrange("(p t) -> p t", t=PACK))
-        b_one = sb([P, PACK], F32, "b_one")
-        nc.gpsimd.tensor_scalar(b_one[:], b_col[:], 1.0, None, ALU.add)
-
+        tab_sc = sb([P, PASSES, T], U8, "tab_sc")
+        nc.vector.memset(tab_sc[:].bitcast(I32), 0)
         wb_sc_raw = sb([P, PASSES, N], U8, "wb_sc_raw")
         nc.vector.memset(wb_sc_raw[:].bitcast(I32), 0)
+        v_sc = sb([P, PASSES, J], U8, "v_sc")
+        nc.vector.memset(v_sc[:].bitcast(I32), 0)
         up_sc_raw = sb([P, N], U8, "up_sc_raw")
-        nc.gpsimd.memset(up_sc_raw[:].bitcast(I32), 0)
+        nc.vector.memset(up_sc_raw[:].bitcast(I32), 0)
+
+        nc.sync.dma_start(dn_raw[0][:, 0:2, :], dn_rows[0][:, 0:2, :])
+        nc.sync.dma_start(tab_sc[4:P:8, :, :].bitcast(I32), tab_scales.rearrange("a s t -> s a t").bitcast(I32))
+        nc.sync.dma_start(dn_raw[0][:, 2:4, :], dn_rows[0][:, 2:4, :])
         for q in range(4):
             nc.sync.dma_start(
                 wb_sc_raw[32 * q : 32 * q + 4, :, :].bitcast(I32),
                 wb_scales[:, 4 * q : 4 * q + 4, :].rearrange("a r n -> r a n").bitcast(I32),
             )
-            nc.gpsimd.dma_start(
-                up_sc_raw[32 * q : 32 * q + 4, :].bitcast(I32), upw_scales[0, 4 * q : 4 * q + 4, :].bitcast(I32)
-            )
+        nc.sync.dma_start(dn_raw[1][:], dn_rows[1])
+        tab_w = sb([P, T], U32, "tab_w")
+        nc.sync.dma_start(tab_w[:].bitcast(I32), tab_words[0].rearrange("p t i -> p (t i)").bitcast(I32))
 
-        g_sc1 = sb([P, J], U8, "g_sc1")
-        nc.vector.memset(g_sc1[:].bitcast(I32), 0)
-        g_sc0 = sb([P, J], U8, "g_sc0")
-        nc.vector.tensor_copy(g_sc0[:], listed(tab_sc[:], 0, J))
-        nc.sync.dma_start(g_sc1[0 : P - 16, :].bitcast(I32), g_sc0[16:P, :].bitcast(I32))
-        g_sc = [g_sc0, g_sc1]
+        g_sc = sb([P, PASSES, J], U8, "g_sc")
+        for a in range(PASSES):
+            nc.vector.tensor_copy(g_sc[:, a, :], listed(tab_sc[:, a, :], 0, J))
+
+        for r in range(PACK):
+            nc.sync.dma_start(v_sc[r:P:32, :, :].bitcast(I32), g_sc[8 * r + 4 : P : 32, :, :].bitcast(I32))
+
+        wb_raw = sb([P, PASSES, N], U32, "wb_raw")
+        nc.sync.dma_start(wb_raw[:].bitcast(I32), wb_words.rearrange("a p n i -> p a (n i)").bitcast(I32))
+        up_raw = sb([P, 2 * N], U8, "up_raw")
+        nc.sync.dma_start(up_raw[:].bitcast(I32), upw_words[0].bitcast(I32))
 
         x_rows = x0T.rearrange("(p t) c -> t p c", t=PACK)
 
@@ -96,10 +88,16 @@ def tile_list_xcross_reluP_kernel(
             nc.sync.dma_start(win[:], x_rows[t])
             return win
 
-        x_win = [load_x(0)]
-        up_raw = sb([P, 2 * N], U8, "up_raw")
-        nc.sync.dma_start(up_raw[:].bitcast(I32), upw_words[0].bitcast(I32))
-        x_win.extend([load_x(t) for t in range(1, PACK)])
+        x_win = [load_x(t) for t in range(PACK)]
+
+        b_col = sb([P, PACK], F32, "b_col")
+        nc.gpsimd.dma_start(b_col[:], b.rearrange("(p t) -> p t", t=PACK))
+        for q in range(4):
+            nc.gpsimd.dma_start(
+                up_sc_raw[32 * q : 32 * q + 4, :].bitcast(I32), upw_scales[0, 4 * q : 4 * q + 4, :].bitcast(I32)
+            )
+        b_one = sb([P, PACK], F32, "b_one")
+        nc.gpsimd.tensor_scalar(b_one[:], b_col[:], 1.0, None, ALU.add)
 
         dn_w, dn_sc = [], []
         for a in range(PASSES):
@@ -108,7 +106,7 @@ def tile_list_xcross_reluP_kernel(
                 grouped[:].rearrange("p (t m i) -> p m i t", t=PACK, i=PACK),
                 dn_raw[a][:].rearrange("p i (m t) -> p m i t", t=PACK),
             )
-            codes = sb([P, R], U32, "dn_w%d" % a, tag=("tab_sc", "dn_w1")[a])
+            codes = sb([P, R], U32, "dn_w%d" % a)
             scales = sb([P, R], U8, "dn_sc%d" % a)
             nc.vector.quantize_mx(out=codes[:].bitcast(FP8X4), scales=scales[:], in_=grouped[:])
             dn_w.append(codes)
@@ -116,7 +114,7 @@ def tile_list_xcross_reluP_kernel(
 
         v_w = []
         for h in range(halves):
-            both = sb([P, HALF], U32, "both%d" % h)
+            both = sb([P, HALF], U32, "both%d" % h, tag="both")
             nc.vector.tensor_copy(both[:], listed(tab_w[:], h * HALF, (h + 1) * HALF))
             parted = sb([P, PASSES, 2 * HALF], U8, "parted%d" % h)
             nc.vector.tensor_copy(
@@ -138,7 +136,7 @@ def tile_list_xcross_reluP_kernel(
         nc.vector.tensor_copy(
             wb_sc[:].rearrange("p a (t m) -> p a m t", t=PACK), wb_sc_raw[:].rearrange("p a (m t) -> p a m t", t=PACK)
         )
-        up_sc = sb([P, N], U8, "up_sc", tag="both1")
+        up_sc = sb([P, N], U8, "up_sc", tag="both")
         nc.vector.tensor_copy(
             up_sc[:].rearrange("p (t m) -> p m t", t=PACK), up_sc_raw[:].rearrange("p (m t) -> p m t", t=PACK)
         )
@@ -156,7 +154,7 @@ def tile_list_xcross_reluP_kernel(
                             lhsT=dn_w[a][:, t * P : (t + 1) * P].bitcast(FP8X4),
                             lhsT_scale=dn_sc[a][:, t * P : (t + 1) * P],
                             rhs=v_w[h][:, a, 2 * c * CHUNK : 2 * (c + 1) * CHUNK].bitcast(FP4X4),
-                            rhs_scale=g_sc[a][:, j0 : j0 + CHUNK],
+                            rhs_scale=v_sc[:, a, j0 : j0 + CHUNK],
                             start=(a == 0),
                             stop=(a == PASSES - 1),
                         )
@@ -183,7 +181,7 @@ def tile_list_xcross_reluP_kernel(
                         lhsT=wb[:, a, rows].bitcast(FP8X4),
                         lhsT_scale=wb_sc[:, a, rows],
                         rhs=v_w[h][:, a, :].bitcast(FP4X4),
-                        rhs_scale=g_sc[a][:, cols],
+                        rhs_scale=v_sc[:, a, cols],
                         start=(a == 0),
                         stop=False,
                     )
@@ -198,42 +196,46 @@ def tile_list_xcross_reluP_kernel(
                 )
                 nc.scalar.activation(z[t][:, cols], bank[:], ACT.Identity, bias=b_one[:, t : t + 1])
 
-        o_lo = sb([P, 2, J], F32, "o_lo")
-        for t in range(2):
-            for h in range(halves):
-                cols = slice(h * HALF, (h + 1) * HALF)
-                nc.vector.tensor_tensor(o_lo[:, t, cols], listed(x_win[t][:], cols.start, cols.stop), z[t][:, cols], ALU.mult)
-
         out_rows = out_0.rearrange("(p t) j -> p t j", t=PACK)
-        nc.sync.dma_start(out_rows[:, 0:2, :], o_lo[:])
-
-        o_bf = [sb([P, PIECE, PACK], BF16, "o_bf%d" % c) for c in range(pieces)]
-        o_hi = [sb([P, 2, PIECE], F32, "o_hi%d" % c) for c in range(pieces)]
-        for c in range(pieces):
-            cols = slice(c * PIECE, (c + 1) * PIECE)
-            nc.scalar.copy(o_bf[c][:, :, 0:2], o_lo[:, :, cols].rearrange("p t j -> p j t"))
-        for c in range(pieces):
-            cols = slice(c * PIECE, (c + 1) * PIECE)
-            nc.vector.tensor_tensor(o_hi[c][:, 0, :], listed(x_win[2][:], cols.start, cols.stop), z[2][:, cols], ALU.mult)
-
-        o_sc = sb([P, J], U8, "o_sc")
         words_out = out_1[0].rearrange("p j i -> p (j i)").bitcast(I32)
-        o_w = [sb([P, PIECE], U32, "o_w%d" % c) for c in range(pieces)]
+        o = sb([P, PACK, J], F32, "o")
+        o_w = sb([P, J], U32, "o_w")
+        o_sc = sb([P, J], U8, "o_sc")
+        cuts = [slice(EDGES[c], EDGES[c + 1]) for c in range(len(EDGES) - 1)]
+        o_bf = [sb([P, cols.stop - cols.start, PACK], BF16, "o_bf%d" % c) for c, cols in enumerate(cuts)]
 
-        def finish(c):
-            cols = slice(c * PIECE, (c + 1) * PIECE)
+        def cross(t, cols):
+            nc.vector.tensor_tensor(o[:, t, cols], listed(x_win[t][:], cols.start, cols.stop), z[t][:, cols], ALU.mult)
+
+        def round_pair(c, t0):
+            nc.scalar.copy(o_bf[c][:, :, t0 : t0 + 2], o[:, t0 : t0 + 2, cuts[c]].rearrange("p t j -> p j t"))
+
+        def quantise(c):
             nc.vector.quantize_mx(
-                out=o_w[c][:].bitcast(FP8X4), scales=o_sc[:, cols], in_=o_bf[c][:].rearrange("p j t -> p (j t)")
+                out=o_w[:, cuts[c]].bitcast(FP8X4), scales=o_sc[:, cuts[c]], in_=o_bf[c][:].rearrange("p j t -> p (j t)")
             )
-            nc.sync.dma_start(words_out[:, cols], o_w[c][:].bitcast(I32))
 
-        for c in range(pieces):
-            cols = slice(c * PIECE, (c + 1) * PIECE)
-            nc.vector.tensor_tensor(o_hi[c][:, 1, :], listed(x_win[3][:], cols.start, cols.stop), z[3][:, cols], ALU.mult)
-            nc.sync.dma_start(out_rows[:, 2:4, cols], o_hi[c][:])
-            nc.scalar.copy(o_bf[c][:, :, 2:4], o_hi[c][:].rearrange("p t j -> p j t"))
+        for t in range(PACK - 1):
+            for h in range(halves):
+                cross(t, slice(h * HALF, (h + 1) * HALF))
+            if t == 1:
+                for c in range(len(cuts)):
+                    round_pair(c, 0)
+        nc.sync.dma_start(out_rows[:, 0:3, :], o[:, 0:3, :])
+
+        early, late = slice(0, STORE_CUT), slice(STORE_CUT, J)
+        for c, cols in enumerate(cuts):
+            cross(3, cols)
+            round_pair(c, 2)
+            if cols.stop == STORE_CUT:
+                nc.sync.dma_start(out_rows[:, 3, early], o[:, 3, early])
             if c > 0:
-                finish(c - 1)
-        finish(pieces - 1)
+                quantise(c - 1)
+                if cols.start == STORE_CUT:
+                    nc.sync.dma_start(words_out[:, early], o_w[:, early].bitcast(I32))
+        nc.sync.dma_start(out_rows[:, 3, late], o[:, 3, late])
+        quantise(len(cuts) - 1)
+        nc.sync.dma_start(words_out[:, late], o_w[:, late].bitcast(I32))
         for q in range(4):
-            nc.scalar.dma_start(out_2[0, 4 * q : 4 * q + 4, :].bitcast(I32), o_sc[32 * q : 32 * q + 4, :].bitcast(I32))
+            queue = nc.sync if q < 2 else nc.scalar
+            queue.dma_start(out_2[0, 4 * q : 4 * q + 4, :].bitcast(I32), o_sc[32 * q : 32 * q + 4, :].bitcast(I32))

@@ -69,6 +69,9 @@ def tile_list_xcross_reluP_kernel(
         tab_w = sb([P, T], U32, "tab_w")
         nc.sync.dma_start(tab_w[:].bitcast(I32), tab_words[0].rearrange("p t i -> p (t i)").bitcast(I32))
 
+        wb_raw = sb([P, PASSES, N], U32, "wb_raw")
+        nc.sync.dma_start(wb_raw[:].bitcast(I32), wb_words.rearrange("a p n i -> p a (n i)").bitcast(I32))
+
         g_sc = sb([P, PASSES, J], U8, "g_sc")
         for a in range(PASSES):
             nc.vector.tensor_copy(g_sc[:, a, :], listed(tab_sc[:, a, :], 0, J))
@@ -76,8 +79,6 @@ def tile_list_xcross_reluP_kernel(
         for r in range(PACK):
             nc.sync.dma_start(v_sc[r:P:32, :, :].bitcast(I32), g_sc[8 * r + 4 : P : 32, :, :].bitcast(I32))
 
-        wb_raw = sb([P, PASSES, N], U32, "wb_raw")
-        nc.sync.dma_start(wb_raw[:].bitcast(I32), wb_words.rearrange("a p n i -> p a (n i)").bitcast(I32))
         up_raw = sb([P, 2 * N], U8, "up_raw")
         nc.sync.dma_start(up_raw[:].bitcast(I32), upw_words[0].bitcast(I32))
 
@@ -207,8 +208,8 @@ def tile_list_xcross_reluP_kernel(
         def cross(t, cols):
             nc.vector.tensor_tensor(o[:, t, cols], listed(x_win[t][:], cols.start, cols.stop), z[t][:, cols], ALU.mult)
 
-        def round_pair(c, t0):
-            nc.scalar.copy(o_bf[c][:, :, t0 : t0 + 2], o[:, t0 : t0 + 2, cuts[c]].rearrange("p t j -> p j t"))
+        def round_pair(c, t0, copy=nc.scalar.copy):
+            copy(o_bf[c][:, :, t0 : t0 + 2], o[:, t0 : t0 + 2, cuts[c]].rearrange("p t j -> p j t"))
 
         def quantise(c):
             nc.vector.quantize_mx(
@@ -219,22 +220,27 @@ def tile_list_xcross_reluP_kernel(
             for h in range(halves):
                 cross(t, slice(h * HALF, (h + 1) * HALF))
             if t == 1:
+                nc.sync.dma_start(out_rows[:, 0:2, :], o[:, 0:2, :])
                 for c in range(len(cuts)):
                     round_pair(c, 0)
-        nc.sync.dma_start(out_rows[:, 0:3, :], o[:, 0:3, :])
+        nc.sync.dma_start(out_rows[:, 2, :], o[:, 2, :])
 
         early, late = slice(0, STORE_CUT), slice(STORE_CUT, J)
-        for c, cols in enumerate(cuts):
-            cross(3, cols)
+        last = len(cuts) - 1
+        for c in range(last):
+            cross(3, cuts[c])
             round_pair(c, 2)
-            if cols.stop == STORE_CUT:
+            if cuts[c].stop == STORE_CUT:
                 nc.sync.dma_start(out_rows[:, 3, early], o[:, 3, early])
-            if c > 0:
+            if 0 < c < last - 1:
                 quantise(c - 1)
-                if cols.start == STORE_CUT:
-                    nc.sync.dma_start(words_out[:, early], o_w[:, early].bitcast(I32))
+        cross(3, cuts[last])
         nc.sync.dma_start(out_rows[:, 3, late], o[:, 3, late])
-        quantise(len(cuts) - 1)
+        quantise(last - 2)
+        nc.sync.dma_start(words_out[:, early], o_w[:, early].bitcast(I32))
+        round_pair(last, 2, nc.vector.tensor_copy)
+        quantise(last - 1)
+        quantise(last)
         nc.sync.dma_start(words_out[:, late], o_w[:, late].bitcast(I32))
         for q in range(4):
             queue = nc.sync if q < 2 else nc.scalar

@@ -1,3 +1,4 @@
+import itertools
 from contextlib import ExitStack
 
 import concourse.mybir as mybir
@@ -103,10 +104,9 @@ def tile_list_xcross_reluP_kernel(
         dn_w, dn_sc = [], []
         for a in range(PASSES):
             grouped = sb([P, PACK * R], BF16, "dn_grouped%d" % a)
-            nc.scalar.copy(
-                grouped[:].rearrange("p (t m i) -> p m i t", t=PACK, i=PACK),
-                dn_raw[a][:].rearrange("p i (m t) -> p m i t", t=PACK),
-            )
+            dealt = grouped[:].rearrange("p (t m i) -> p m i t", t=PACK, i=PACK)
+            rows = dn_raw[a][:].rearrange("p i (m t) -> p m i t", t=PACK)
+            nc.scalar.copy(dealt, rows)
             codes = sb([P, R], U32, "dn_w%d" % a)
             scales = sb([P, R], U8, "dn_sc%d" % a)
             nc.vector.quantize_mx(out=codes[:].bitcast(FP8X4), scales=scales[:], in_=grouped[:])
@@ -169,11 +169,17 @@ def tile_list_xcross_reluP_kernel(
             nc.vector.quantize_mx(out=codes[:].bitcast(FP8X4), scales=scales[:], in_=h_bf[:])
             h_w.append(codes)
             h_sc.append(scales)
+            if h == 0:
+                x_first = sb([P, J], F32, "x_first", tag="h_bf0")
+                for part in range(halves):
+                    cols = slice(part * HALF, (part + 1) * HALF)
+                    nc.vector.tensor_copy(x_first[:, cols], listed(x_win[0][:], cols.start, cols.stop))
 
-        z = [sb([P, J], F32, "z%d" % t) for t in range(PACK)]
-        for t in range(PACK):
-            rows = slice(t * P, (t + 1) * P)
-            for h in range(halves):
+        o = sb([P, PACK, J], F32, "o")
+        z = {t: sb([P, J], F32, "z%d" % t) for t in range(1, PACK)}
+        for pair in range(2):
+            for h, t in itertools.product(range(halves), (2 * pair, 2 * pair + 1)):
+                rows = slice(t * P, (t + 1) * P)
                 cols = slice(h * HALF, (h + 1) * HALF)
                 bank = psum.tile([P, HALF], F32, name="y%d_%d" % (t, h), tag="bank%d" % (halves * t + h))
                 for a in range(PASSES):
@@ -195,11 +201,17 @@ def tile_list_xcross_reluP_kernel(
                     start=False,
                     stop=True,
                 )
-                nc.scalar.activation(z[t][:, cols], bank[:], ACT.Identity, bias=b_one[:, t : t + 1])
+                if t == 0:
+                    nc.vector.scalar_tensor_tensor(
+                        o[:, 0, cols], bank[:], b_one[:, 0:1], x_first[:, cols], ALU.add, ALU.mult
+                    )
+                else:
+                    nc.scalar.activation(z[t][:, cols], bank[:], ACT.Identity, bias=b_one[:, t : t + 1])
+                if t == 1:
+                    nc.vector.tensor_tensor(o[:, 1, cols], listed(x_win[1][:], cols.start, cols.stop), z[1][:, cols], ALU.mult)
 
         out_rows = out_0.rearrange("(p t) j -> p t j", t=PACK)
         words_out = out_1[0].rearrange("p j i -> p (j i)").bitcast(I32)
-        o = sb([P, PACK, J], F32, "o")
         o_w = sb([P, J], U32, "o_w")
         o_sc = sb([P, J], U8, "o_sc")
         cuts = [slice(EDGES[c], EDGES[c + 1]) for c in range(len(EDGES) - 1)]
@@ -216,13 +228,13 @@ def tile_list_xcross_reluP_kernel(
                 out=o_w[:, cuts[c]].bitcast(FP8X4), scales=o_sc[:, cuts[c]], in_=o_bf[c][:].rearrange("p j t -> p (j t)")
             )
 
-        for t in range(PACK - 1):
-            for h in range(halves):
-                cross(t, slice(h * HALF, (h + 1) * HALF))
-            if t == 1:
-                nc.sync.dma_start(out_rows[:, 0:2, :], o[:, 0:2, :])
-                for c in range(len(cuts)):
-                    round_pair(c, 0)
+        nc.sync.dma_start(out_rows[:, 0:2, :], o[:, 0:2, :])
+        for c in range(len(cuts) - 2):
+            round_pair(c, 0)
+        for c in range(len(cuts) - 2, len(cuts)):
+            round_pair(c, 0, nc.vector.tensor_copy)
+        for h in range(halves):
+            cross(2, slice(h * HALF, (h + 1) * HALF))
         nc.sync.dma_start(out_rows[:, 2, :], o[:, 2, :])
 
         early, late = slice(0, STORE_CUT), slice(STORE_CUT, J)

@@ -22,8 +22,9 @@ PACK = 4
 PASSES = K // (P * PACK)
 HALF = 512
 CHUNK = 128
-EDGES = (0, 128, 384, 640, 896, 1024)
+EDGES = (0, 128, 384, 640, 768, 896, 1024)
 STORE_CUT = 640
+WORDS_CUT = 640
 LIST_ROWS = 16
 
 
@@ -72,6 +73,8 @@ def tile_list_xcross_reluP_kernel(
 
         wb_raw = sb([P, PASSES, N], U32, "wb_raw")
         nc.sync.dma_start(wb_raw[:].bitcast(I32), wb_words.rearrange("a p n i -> p a (n i)").bitcast(I32))
+        up_raw = sb([P, 2 * N], U8, "up_raw")
+        nc.sync.dma_start(up_raw[:].bitcast(I32), upw_words[0].bitcast(I32))
 
         g_sc = sb([P, PASSES, J], U8, "g_sc")
         for a in range(PASSES):
@@ -80,8 +83,6 @@ def tile_list_xcross_reluP_kernel(
         for r in range(PACK):
             nc.sync.dma_start(v_sc[r:P:32, :, :].bitcast(I32), g_sc[8 * r + 4 : P : 32, :, :].bitcast(I32))
 
-        up_raw = sb([P, 2 * N], U8, "up_raw")
-        nc.sync.dma_start(up_raw[:].bitcast(I32), upw_words[0].bitcast(I32))
 
         x_rows = x0T.rearrange("(p t) c -> t p c", t=PACK)
 
@@ -229,9 +230,9 @@ def tile_list_xcross_reluP_kernel(
             )
 
         nc.sync.dma_start(out_rows[:, 0:2, :], o[:, 0:2, :])
-        for c in range(len(cuts) - 2):
+        for c in range(3):
             round_pair(c, 0)
-        for c in range(len(cuts) - 2, len(cuts)):
+        for c in range(3, len(cuts)):
             round_pair(c, 0, nc.vector.tensor_copy)
         for h in range(halves):
             cross(2, slice(h * HALF, (h + 1) * HALF))
@@ -248,12 +249,12 @@ def tile_list_xcross_reluP_kernel(
                 quantise(c - 1)
         cross(3, cuts[last])
         nc.sync.dma_start(out_rows[:, 3, late], o[:, 3, late])
+        nc.sync.dma_start(words_out[:, 0:WORDS_CUT], o_w[:, 0:WORDS_CUT].bitcast(I32))
         quantise(last - 2)
-        nc.sync.dma_start(words_out[:, early], o_w[:, early].bitcast(I32))
         round_pair(last, 2, nc.vector.tensor_copy)
         quantise(last - 1)
         quantise(last)
-        nc.sync.dma_start(words_out[:, late], o_w[:, late].bitcast(I32))
+        nc.sync.dma_start(words_out[:, WORDS_CUT:J], o_w[:, WORDS_CUT:J].bitcast(I32))
         for q in range(4):
             queue = nc.sync if q < 2 else nc.scalar
             queue.dma_start(out_2[0, 4 * q : 4 * q + 4, :].bitcast(I32), o_sc[32 * q : 32 * q + 4, :].bitcast(I32))

@@ -26,6 +26,9 @@ EDGES = (0, 128, 384, 640, 768, 896, 1024)
 STORE_CUT = 640
 WORDS_CUT = 640
 LIST_ROWS = 16
+AT_EARLY = 0
+AT_LATE = AT_EARLY + 2 * PACK * STORE_CUT
+Y_BANKS = (0, 1, 2, 1, 0, 2, 1, 0)
 
 
 def tile_list_xcross_reluP_kernel(
@@ -36,10 +39,14 @@ def tile_list_xcross_reluP_kernel(
 
     with ExitStack() as ctx:
         keep = ctx.enter_context(tc.tile_pool(name="keep", bufs=1))
+        reuse = ctx.enter_context(tc.tile_pool(name="reuse", bufs=1))
         psum = ctx.enter_context(tc.psum_pool(name="psum", bufs=1))
 
         def sb(shape, dtype, name, tag=None):
             return keep.tile(shape, dtype, name=name, tag=tag or name, align_bytes=64)
+
+        def at(offset, shape, dtype, name):
+            return reuse.tile(shape, dtype, name=name, align_bytes=64, offset=offset)
 
         def listed(window, j0, j1):
             return window.indirect(offsets[:, j0 // LIST_ROWS : j1 // LIST_ROWS])
@@ -50,7 +57,7 @@ def tile_list_xcross_reluP_kernel(
         dn_rows = dn.rearrange("(a p i) r -> a p i r", a=PASSES, i=PACK)
         dn_raw = [sb([P, PACK, R], F32, "dn_raw%d" % a) for a in range(PASSES)]
 
-        tab_sc = sb([P, PASSES, T], U8, "tab_sc")
+        tab_sc = sb([P, T], U8, "tab_sc")
         nc.vector.memset(tab_sc[:].bitcast(I32), 0)
         wb_sc_raw = sb([P, PASSES, N], U8, "wb_sc_raw")
         nc.vector.memset(wb_sc_raw[:].bitcast(I32), 0)
@@ -60,7 +67,7 @@ def tile_list_xcross_reluP_kernel(
         nc.vector.memset(up_sc_raw[:].bitcast(I32), 0)
 
         nc.sync.dma_start(dn_raw[0][:, 0:2, :], dn_rows[0][:, 0:2, :])
-        nc.sync.dma_start(tab_sc[4:P:8, :, :].bitcast(I32), tab_scales.rearrange("a s t -> s a t").bitcast(I32))
+        nc.sync.dma_start(tab_sc[0:P:4, :].bitcast(I32), tab_scales.rearrange("a s t -> (a s) t").bitcast(I32))
         nc.sync.dma_start(dn_raw[0][:, 2:4, :], dn_rows[0][:, 2:4, :])
         for q in range(4):
             nc.sync.dma_start(
@@ -69,20 +76,23 @@ def tile_list_xcross_reluP_kernel(
             )
         nc.sync.dma_start(dn_raw[1][:], dn_rows[1])
         tab_w = sb([P, T], U32, "tab_w")
-        nc.sync.dma_start(tab_w[:].bitcast(I32), tab_words[0].rearrange("p t i -> p (t i)").bitcast(I32))
+        tab_rows = tab_words[0].rearrange("p t i -> p (t i)").bitcast(I32)
+        g_sc = sb([P, J], U8, "g_sc")
+        nc.vector.tensor_copy(g_sc[:], listed(tab_sc[:], 0, J))
 
+        def move_scales(a):
+            for r in range(PACK):
+                first = 64 * a + 4 * r
+                nc.sync.dma_start(v_sc[r:P:32, a, :].bitcast(I32), g_sc[first : first + 49 : 16, :].bitcast(I32))
+
+        nc.sync.dma_start(tab_w[:, 0 : T // 2].bitcast(I32), tab_rows[:, 0 : T // 2])
+        move_scales(0)
+        nc.sync.dma_start(tab_w[:, T // 2 : T].bitcast(I32), tab_rows[:, T // 2 : T])
         wb_raw = sb([P, PASSES, N], U32, "wb_raw")
         nc.sync.dma_start(wb_raw[:].bitcast(I32), wb_words.rearrange("a p n i -> p a (n i)").bitcast(I32))
+        move_scales(1)
         up_raw = sb([P, 2 * N], U8, "up_raw")
         nc.sync.dma_start(up_raw[:].bitcast(I32), upw_words[0].bitcast(I32))
-
-        g_sc = sb([P, PASSES, J], U8, "g_sc")
-        for a in range(PASSES):
-            nc.vector.tensor_copy(g_sc[:, a, :], listed(tab_sc[:, a, :], 0, J))
-
-        for r in range(PACK):
-            nc.sync.dma_start(v_sc[r:P:32, :, :].bitcast(I32), g_sc[8 * r + 4 : P : 32, :, :].bitcast(I32))
-
 
         x_rows = x0T.rearrange("(p t) c -> t p c", t=PACK)
 
@@ -99,8 +109,11 @@ def tile_list_xcross_reluP_kernel(
             nc.gpsimd.dma_start(
                 up_sc_raw[32 * q : 32 * q + 4, :].bitcast(I32), upw_scales[0, 4 * q : 4 * q + 4, :].bitcast(I32)
             )
-        b_one = sb([P, PACK], F32, "b_one")
-        nc.gpsimd.tensor_scalar(b_one[:], b_col[:], 1.0, None, ALU.add)
+        b_low = at(AT_EARLY, [P, PACK - 1], F32, "b_low")
+        nc.gpsimd.tensor_scalar(b_low[:], b_col[:, 0 : PACK - 1], 1.0, None, ALU.add)
+        b_high = sb([P, 1], F32, "b_high")
+        nc.gpsimd.tensor_scalar(b_high[:], b_col[:, PACK - 1 : PACK], 1.0, None, ALU.add)
+        b_one = [b_low[:, t : t + 1] for t in range(PACK - 1)] + [b_high[:]]
 
         dn_w, dn_sc = [], []
         for a in range(PASSES):
@@ -119,9 +132,11 @@ def tile_list_xcross_reluP_kernel(
             both = sb([P, HALF], U32, "both%d" % h, tag="both")
             nc.vector.tensor_copy(both[:], listed(tab_w[:], h * HALF, (h + 1) * HALF))
             parted = sb([P, PASSES, 2 * HALF], U8, "parted%d" % h)
-            nc.vector.tensor_copy(
-                parted[:].bitcast(U16), both[:].bitcast(U16).rearrange("p (j a) -> p a j", a=PASSES)
-            )
+            for cols in (slice(0, CHUNK), slice(CHUNK, HALF)) if h == 0 else (slice(0, HALF),):
+                nc.vector.tensor_copy(
+                    parted[:].bitcast(U16)[:, :, cols],
+                    both[:].bitcast(U16).rearrange("p (j a) -> p a j", a=PASSES)[:, :, cols],
+                )
             v_w.append(parted)
 
         wb = sb([P, PASSES, N], U32, "wb")
@@ -177,12 +192,13 @@ def tile_list_xcross_reluP_kernel(
                     nc.vector.tensor_copy(x_first[:, cols], listed(x_win[0][:], cols.start, cols.stop))
 
         o = sb([P, PACK, J], F32, "o")
-        z = {t: sb([P, J], F32, "z%d" % t) for t in range(1, PACK)}
+        z = {t: at(AT_LATE, [P, J], F32, "z2") if t == 2 else sb([P, J], F32, "z%d" % t) for t in range(1, PACK)}
         for pair in range(2):
-            for h, t in itertools.product(range(halves), (2 * pair, 2 * pair + 1)):
+            order = itertools.product(range(halves), (0, 1)) if pair == 0 else ((0, 2), (1, 2), (0, 3), (1, 3))
+            for turn, (h, t) in enumerate(order):
                 rows = slice(t * P, (t + 1) * P)
                 cols = slice(h * HALF, (h + 1) * HALF)
-                bank = psum.tile([P, HALF], F32, name="y%d_%d" % (t, h), tag="bank%d" % (halves * t + h))
+                bank = psum.tile([P, HALF], F32, name="y%d_%d" % (t, h), tag="bank%d" % Y_BANKS[4 * pair + turn])
                 for a in range(PASSES):
                     nc.tensor.matmul_mx(
                         out=bank[:],
@@ -204,10 +220,10 @@ def tile_list_xcross_reluP_kernel(
                 )
                 if t == 0:
                     nc.vector.scalar_tensor_tensor(
-                        o[:, 0, cols], bank[:], b_one[:, 0:1], x_first[:, cols], ALU.add, ALU.mult
+                        o[:, 0, cols], bank[:], b_one[0], x_first[:, cols], ALU.add, ALU.mult
                     )
                 else:
-                    nc.scalar.activation(z[t][:, cols], bank[:], ACT.Identity, bias=b_one[:, t : t + 1])
+                    nc.scalar.activation(z[t][:, cols], bank[:], ACT.Identity, bias=b_one[t])
                 if t == 1:
                     nc.vector.tensor_tensor(o[:, 1, cols], listed(x_win[1][:], cols.start, cols.stop), z[1][:, cols], ALU.mult)
 
@@ -216,7 +232,12 @@ def tile_list_xcross_reluP_kernel(
         o_w = sb([P, J], U32, "o_w")
         o_sc = sb([P, J], U8, "o_sc")
         cuts = [slice(EDGES[c], EDGES[c + 1]) for c in range(len(EDGES) - 1)]
-        o_bf = [sb([P, cols.stop - cols.start, PACK], BF16, "o_bf%d" % c) for c, cols in enumerate(cuts)]
+        o_early = at(AT_EARLY, [P, STORE_CUT, PACK], BF16, "o_early")
+        o_late = at(AT_LATE, [P, J - STORE_CUT, PACK], BF16, "o_late")
+        o_bf = [
+            o_early[:, cols, :] if cols.stop <= STORE_CUT else o_late[:, cols.start - STORE_CUT : cols.stop - STORE_CUT, :]
+            for cols in cuts
+        ]
 
         def cross(t, cols):
             nc.vector.tensor_tensor(o[:, t, cols], listed(x_win[t][:], cols.start, cols.stop), z[t][:, cols], ALU.mult)
@@ -226,16 +247,13 @@ def tile_list_xcross_reluP_kernel(
 
         def quantise(c):
             nc.vector.quantize_mx(
-                out=o_w[:, cuts[c]].bitcast(FP8X4), scales=o_sc[:, cuts[c]], in_=o_bf[c][:].rearrange("p j t -> p (j t)")
+                out=o_w[:, cuts[c]].bitcast(FP8X4), scales=o_sc[:, cuts[c]], in_=o_bf[c].rearrange("p j t -> p (j t)")
             )
 
         nc.sync.dma_start(out_rows[:, 0:2, :], o[:, 0:2, :])
-        for c in range(3):
-            round_pair(c, 0)
-        for c in range(3, len(cuts)):
-            round_pair(c, 0, nc.vector.tensor_copy)
-        for h in range(halves):
-            cross(2, slice(h * HALF, (h + 1) * HALF))
+        nc.scalar.copy(o_early[:, :, 0:2], o[:, 0:2, 0:STORE_CUT].rearrange("p t j -> p j t"))
+        cross(2, slice(0, J))
+        nc.vector.tensor_copy(o_late[:, :, 0:2], o[:, 0:2, STORE_CUT:J].rearrange("p t j -> p j t"))
         nc.sync.dma_start(out_rows[:, 2, :], o[:, 2, :])
 
         early, late = slice(0, STORE_CUT), slice(STORE_CUT, J)

@@ -52,47 +52,56 @@ def tile_list_xcross_reluP_kernel(
             return window.indirect(offsets[:, j0 // LIST_ROWS : j1 // LIST_ROWS])
 
         offsets = keep.tile([P, J // LIST_ROWS], U16, name="offsets")
-        nc.sync.dma_start(offsets[:], offs)
 
         dn_rows = dn.rearrange("(a p i) r -> a p i r", a=PASSES, i=PACK)
         dn_raw = [sb([P, PACK, R], F32, "dn_raw%d" % a) for a in range(PASSES)]
 
         tab_sc = sb([P, T], U8, "tab_sc")
         nc.vector.memset(tab_sc[:].bitcast(I32), 0)
-        wb_sc_raw = sb([P, PASSES, N], U8, "wb_sc_raw")
-        nc.vector.memset(wb_sc_raw[:].bitcast(I32), 0)
-        v_sc = sb([P, PASSES, J], U8, "v_sc")
-        nc.vector.memset(v_sc[:].bitcast(I32), 0)
-        up_sc_raw = sb([P, N], U8, "up_sc_raw")
-        nc.vector.memset(up_sc_raw[:].bitcast(I32), 0)
+        w_sc_raw = sb([P, PASSES + 1, N], U8, "w_sc_raw")
+        nc.vector.memset(w_sc_raw[:].bitcast(I32), 0)
+        plane0 = sb([P, J], U8, "plane0")
+        nc.vector.memset(plane0[:].bitcast(I32), 0)
+        plane1 = sb([P, J + (PASSES + 1) * N], U8, "plane1")
+        nc.vector.memset(plane1[:].bitcast(I32), 0)
+        v_sc = [plane0, plane1]
+        b_rows = sb([P, P], F32, "b_rows")
+        nc.vector.memset(b_rows[:], 0.0)
 
         nc.sync.dma_start(dn_raw[0][:, 0:2, :], dn_rows[0][:, 0:2, :])
+        nc.sync.dma_start(offsets[:], offs)
         nc.sync.dma_start(tab_sc[0:P:4, :].bitcast(I32), tab_scales.rearrange("a s t -> (a s) t").bitcast(I32))
         nc.sync.dma_start(dn_raw[0][:, 2:4, :], dn_rows[0][:, 2:4, :])
-        for q in range(4):
-            nc.sync.dma_start(
-                wb_sc_raw[32 * q : 32 * q + 4, :, :].bitcast(I32),
-                wb_scales[:, 4 * q : 4 * q + 4, :].rearrange("a r n -> r a n").bitcast(I32),
-            )
+        nc.sync.dma_start(w_sc_raw[64:P:4, 0:PASSES, :].bitcast(I32), wb_scales.rearrange("a s n -> s a n").bitcast(I32))
+        nc.sync.dma_start(w_sc_raw[64:P:4, PASSES, :].bitcast(I32), upw_scales[0].bitcast(I32))
         nc.sync.dma_start(dn_raw[1][:], dn_rows[1])
+        nc.sync.dma_start(b_rows[0:P:32, :], b.rearrange("(q c) -> q c", q=4))
         tab_w = sb([P, T], U32, "tab_w")
         tab_rows = tab_words[0].rearrange("p t i -> p (t i)").bitcast(I32)
         g_sc = sb([P, J], U8, "g_sc")
         nc.vector.tensor_copy(g_sc[:], listed(tab_sc[:], 0, J))
 
+        staged = sb([P, J + (PASSES + 1) * N], U8, "staged")
+        nc.vector.tensor_copy(staged[:, 0:J].bitcast(I32), g_sc[:].bitcast(I32))
+        nc.vector.tensor_copy(
+            staged[:, J:].rearrange("p (a t m) -> p a m t", a=PASSES + 1, t=PACK),
+            w_sc_raw[:].rearrange("p a (m t) -> p a m t", t=PACK),
+        )
+
         def move_scales(a):
+            source = (g_sc, staged)[a]
             for r in range(PACK):
                 first = 64 * a + 4 * r
-                nc.sync.dma_start(v_sc[r:P:32, a, :].bitcast(I32), g_sc[first : first + 49 : 16, :].bitcast(I32))
+                nc.sync.dma_start(v_sc[a][r:P:32, :].bitcast(I32), source[first : first + 49 : 16, :].bitcast(I32))
 
         nc.sync.dma_start(tab_w[:, 0 : T // 2].bitcast(I32), tab_rows[:, 0 : T // 2])
         move_scales(0)
         nc.sync.dma_start(tab_w[:, T // 2 : T].bitcast(I32), tab_rows[:, T // 2 : T])
         wb_raw = sb([P, PASSES, N], U32, "wb_raw")
         nc.sync.dma_start(wb_raw[:].bitcast(I32), wb_words.rearrange("a p n i -> p a (n i)").bitcast(I32))
-        move_scales(1)
         up_raw = sb([P, 2 * N], U8, "up_raw")
         nc.sync.dma_start(up_raw[:].bitcast(I32), upw_words[0].bitcast(I32))
+        move_scales(1)
 
         x_rows = x0T.rearrange("(p t) c -> t p c", t=PACK)
 
@@ -103,17 +112,15 @@ def tile_list_xcross_reluP_kernel(
 
         x_win = [load_x(t) for t in range(PACK)]
 
-        b_col = sb([P, PACK], F32, "b_col")
-        nc.gpsimd.dma_start(b_col[:], b.rearrange("(p t) -> p t", t=PACK))
-        for q in range(4):
-            nc.gpsimd.dma_start(
-                up_sc_raw[32 * q : 32 * q + 4, :].bitcast(I32), upw_scales[0, 4 * q : 4 * q + 4, :].bitcast(I32)
-            )
+        b_dealt = sb([P, P], F32, "b_dealt")
+        nc.vector.tensor_scalar(
+            b_dealt[:].rearrange("p (t m) -> p t m", t=PACK), b_rows[:].rearrange("p (m t) -> p t m", t=PACK), 1.0, None, ALU.add
+        )
+        b_turned = sb([P, P], F32, "b_turned")
+        nc.vector.transpose(b_turned[:], b_dealt[:])
         b_low = at(AT_EARLY, [P, PACK - 1], F32, "b_low")
-        nc.gpsimd.tensor_scalar(b_low[:], b_col[:, 0 : PACK - 1], 1.0, None, ALU.add)
-        b_high = sb([P, 1], F32, "b_high")
-        nc.gpsimd.tensor_scalar(b_high[:], b_col[:, PACK - 1 : PACK], 1.0, None, ALU.add)
-        b_one = [b_low[:, t : t + 1] for t in range(PACK - 1)] + [b_high[:]]
+        nc.vector.tensor_copy(b_low[:], b_turned[:, 0:96:32])
+        b_one = [b_low[:, t : t + 1] for t in range(PACK - 1)] + [b_turned[:, 96:97]]
 
         dn_w, dn_sc = [], []
         for a in range(PASSES):
@@ -149,14 +156,6 @@ def tile_list_xcross_reluP_kernel(
             up[:].bitcast(U16).rearrange("p (t m) -> p m t", t=PACK),
             up_raw[:].bitcast(U16).rearrange("p (m t) -> p m t", t=PACK),
         )
-        wb_sc = sb([P, PASSES, N], U8, "wb_sc")
-        nc.vector.tensor_copy(
-            wb_sc[:].rearrange("p a (t m) -> p a m t", t=PACK), wb_sc_raw[:].rearrange("p a (m t) -> p a m t", t=PACK)
-        )
-        up_sc = sb([P, N], U8, "up_sc", tag="both")
-        nc.vector.tensor_copy(
-            up_sc[:].rearrange("p (t m) -> p m t", t=PACK), up_sc_raw[:].rearrange("p (m t) -> p m t", t=PACK)
-        )
 
         h_w, h_sc = [], []
         for h in range(halves):
@@ -171,7 +170,7 @@ def tile_list_xcross_reluP_kernel(
                             lhsT=dn_w[a][:, t * P : (t + 1) * P].bitcast(FP8X4),
                             lhsT_scale=dn_sc[a][:, t * P : (t + 1) * P],
                             rhs=v_w[h][:, a, 2 * c * CHUNK : 2 * (c + 1) * CHUNK].bitcast(FP4X4),
-                            rhs_scale=v_sc[:, a, j0 : j0 + CHUNK],
+                            rhs_scale=v_sc[a][:, j0 : j0 + CHUNK],
                             start=(a == 0),
                             stop=(a == PASSES - 1),
                         )
@@ -203,16 +202,16 @@ def tile_list_xcross_reluP_kernel(
                     nc.tensor.matmul_mx(
                         out=bank[:],
                         lhsT=wb[:, a, rows].bitcast(FP8X4),
-                        lhsT_scale=wb_sc[:, a, rows],
+                        lhsT_scale=plane1[:, J + a * N + rows.start : J + a * N + rows.stop],
                         rhs=v_w[h][:, a, :].bitcast(FP4X4),
-                        rhs_scale=v_sc[:, a, cols],
+                        rhs_scale=v_sc[a][:, cols],
                         start=(a == 0),
                         stop=False,
                     )
                 nc.tensor.matmul_mx(
                     out=bank[:],
                     lhsT=up[:, 2 * t * P : 2 * (t + 1) * P].bitcast(FP4X4),
-                    lhsT_scale=up_sc[:, rows],
+                    lhsT_scale=plane1[:, J + PASSES * N + rows.start : J + PASSES * N + rows.stop],
                     rhs=h_w[h][:].bitcast(FP8X4),
                     rhs_scale=h_sc[h][:],
                     start=False,

@@ -26,6 +26,8 @@ EDGES = (0, 128, 384, 640, 768, 896, 1024)
 STORE_CUT = 640
 WORDS_CUT = 640
 LIST_ROWS = 16
+TAB_CUT = 2304
+X_CUT = 512
 AT_EARLY = 0
 AT_LATE = AT_EARLY + 2 * PACK * STORE_CUT
 Y_BANKS = (0, 1, 2, 1, 0, 2, 1, 0)
@@ -94,23 +96,21 @@ def tile_list_xcross_reluP_kernel(
                 first = 64 * a + 4 * r
                 nc.sync.dma_start(v_sc[a][r:P:32, :].bitcast(I32), source[first : first + 49 : 16, :].bitcast(I32))
 
-        nc.sync.dma_start(tab_w[:, 0 : T // 2].bitcast(I32), tab_rows[:, 0 : T // 2])
-        move_scales(0)
-        nc.sync.dma_start(tab_w[:, T // 2 : T].bitcast(I32), tab_rows[:, T // 2 : T])
-        wb_raw = sb([P, PASSES, N], U32, "wb_raw")
-        nc.sync.dma_start(wb_raw[:].bitcast(I32), wb_words.rearrange("a p n i -> p a (n i)").bitcast(I32))
+        nc.sync.dma_start(tab_w[:, 0:TAB_CUT].bitcast(I32), tab_rows[:, 0:TAB_CUT])
         up_raw = sb([P, 2 * N], U8, "up_raw")
         nc.sync.dma_start(up_raw[:].bitcast(I32), upw_words[0].bitcast(I32))
-        move_scales(1)
+        move_scales(0)
+        nc.sync.dma_start(tab_w[:, TAB_CUT:T].bitcast(I32), tab_rows[:, TAB_CUT:T])
+        wb_raw = sb([P, PASSES, N], U32, "wb_raw")
+        nc.sync.dma_start(wb_raw[:].bitcast(I32), wb_words.rearrange("a p n i -> p a (n i)").bitcast(I32))
 
         x_rows = x0T.rearrange("(p t) c -> t p c", t=PACK)
-
-        def load_x(t):
-            win = sb([P, T], F32, "x_win%d" % t)
-            nc.sync.dma_start(win[:], x_rows[t])
-            return win
-
-        x_win = [load_x(t) for t in range(PACK)]
+        x_win = [sb([P, T], F32, "x_win%d" % t) for t in range(PACK)]
+        nc.sync.dma_start(x_win[0][:, 0:X_CUT], x_rows[0][:, 0:X_CUT])
+        move_scales(1)
+        nc.sync.dma_start(x_win[0][:, X_CUT:T], x_rows[0][:, X_CUT:T])
+        for t in range(1, PACK):
+            nc.sync.dma_start(x_win[t][:], x_rows[t])
 
         b_dealt = sb([P, P], F32, "b_dealt")
         nc.vector.tensor_scalar(

@@ -1,4 +1,3 @@
-import itertools
 from contextlib import ExitStack
 
 import concourse.mybir as mybir
@@ -19,36 +18,35 @@ ALU = mybir.AluOpType
 
 P = 128
 PACK = 4
+QUADRANT = 32
 PASSES = K // (P * PACK)
 HALF = 512
+HALVES = J // HALF
 CHUNK = 128
-EDGES = (0, 128, 384, 640, 768, 896, 1024)
-STORE_CUT = 640
-WORDS_CUT = 640
 LIST_ROWS = 16
-TAB_CUT = 2304
-X_CUT = 512
-AT_EARLY = 0
-AT_LATE = AT_EARLY + 2 * PACK * STORE_CUT
-Y_BANKS = (0, 1, 2, 1, 0, 2, 1, 0)
+SPREAD = 4
+PASS_SPAN = 64
+HS_BANK = 4
+EDGES = (0, 128, 384, 640, 768, 896, 1024)
+CUT = 640
+
+
+def y_bank(t, h):
+    return 2 * h + (0, 1, 1)[t] if t < PACK - 1 else 2 * (1 - h)
 
 
 def tile_list_xcross_reluP_kernel(
     tc, tab_words, tab_scales, wb_words, wb_scales, dn, upw_words, upw_scales, x0T, b, offs, out_0, out_1, out_2
 ):
     nc = tc.nc
-    halves = J // HALF
 
     with ExitStack() as ctx:
         keep = ctx.enter_context(tc.tile_pool(name="keep", bufs=1))
-        reuse = ctx.enter_context(tc.tile_pool(name="reuse", bufs=1))
+        shared = ctx.enter_context(tc.tile_pool(name="shared", bufs=1))
         psum = ctx.enter_context(tc.psum_pool(name="psum", bufs=1))
 
         def sb(shape, dtype, name, tag=None):
             return keep.tile(shape, dtype, name=name, tag=tag or name, align_bytes=64)
-
-        def at(offset, shape, dtype, name):
-            return reuse.tile(shape, dtype, name=name, align_bytes=64, offset=offset)
 
         def listed(window, j0, j1):
             return window.indirect(offsets[:, j0 // LIST_ROWS : j1 // LIST_ROWS])
@@ -56,7 +54,8 @@ def tile_list_xcross_reluP_kernel(
         offsets = keep.tile([P, J // LIST_ROWS], U16, name="offsets")
 
         dn_rows = dn.rearrange("(a p i) r -> a p i r", a=PASSES, i=PACK)
-        dn_raw = [sb([P, PACK, R], F32, "dn_raw%d" % a) for a in range(PASSES)]
+        dn_first = sb([P, PACK, R], F32, "dn_raw0")
+        dn_late = [sb([P, 2, R], F32, "dn_late%d" % u) for u in range(2)]
 
         tab_sc = sb([P, T], U8, "tab_sc")
         nc.vector.memset(tab_sc[:].bitcast(I32), 0)
@@ -70,19 +69,20 @@ def tile_list_xcross_reluP_kernel(
         b_rows = sb([P, P], F32, "b_rows")
         nc.vector.memset(b_rows[:], 0.0)
 
-        nc.sync.dma_start(dn_raw[0][:, 0:2, :], dn_rows[0][:, 0:2, :])
+        nc.sync.dma_start(dn_first[:, 0:2, :], dn_rows[0][:, 0:2, :])
         nc.sync.dma_start(offsets[:], offs)
-        nc.sync.dma_start(tab_sc[0:P:4, :].bitcast(I32), tab_scales.rearrange("a s t -> (a s) t").bitcast(I32))
-        nc.sync.dma_start(dn_raw[0][:, 2:4, :], dn_rows[0][:, 2:4, :])
-        nc.sync.dma_start(w_sc_raw[64:P:4, 0:PASSES, :].bitcast(I32), wb_scales.rearrange("a s n -> s a n").bitcast(I32))
-        nc.sync.dma_start(w_sc_raw[64:P:4, PASSES, :].bitcast(I32), upw_scales[0].bitcast(I32))
-        nc.sync.dma_start(dn_raw[1][:], dn_rows[1])
-        nc.sync.dma_start(b_rows[0:P:32, :], b.rearrange("(q c) -> q c", q=4))
+        nc.sync.dma_start(tab_sc[0:P:SPREAD, :].bitcast(I32), tab_scales.rearrange("a s t -> (a s) t").bitcast(I32))
+        nc.sync.dma_start(dn_first[:, 2:4, :], dn_rows[0][:, 2:4, :])
+        nc.sync.dma_start(
+            w_sc_raw[PASS_SPAN:P:SPREAD, 0:PASSES, :].bitcast(I32), wb_scales.rearrange("a s n -> s a n").bitcast(I32)
+        )
+        nc.sync.dma_start(w_sc_raw[PASS_SPAN:P:SPREAD, PASSES, :].bitcast(I32), upw_scales[0].bitcast(I32))
+        nc.sync.dma_start(b_rows[0:P:QUADRANT, :], b.rearrange("(q c) -> q c", c=P))
         tab_w = sb([P, T], U32, "tab_w")
         tab_rows = tab_words[0].rearrange("p t i -> p (t i)").bitcast(I32)
+
         g_sc = sb([P, J], U8, "g_sc")
         nc.vector.tensor_copy(g_sc[:], listed(tab_sc[:], 0, J))
-
         staged = sb([P, J + (PASSES + 1) * N], U8, "staged")
         nc.vector.tensor_copy(staged[:, 0:J].bitcast(I32), g_sc[:].bitcast(I32))
         nc.vector.tensor_copy(
@@ -92,61 +92,74 @@ def tile_list_xcross_reluP_kernel(
 
         def move_scales(a):
             source = (g_sc, staged)[a]
+            step = PACK * SPREAD
             for r in range(PACK):
-                first = 64 * a + 4 * r
-                nc.sync.dma_start(v_sc[a][r:P:32, :].bitcast(I32), source[first : first + 49 : 16, :].bitcast(I32))
+                first = PASS_SPAN * a + SPREAD * r
+                rows = source[first : first + (PACK - 1) * step + 1 : step, :]
+                nc.sync.dma_start(v_sc[a][r:P:QUADRANT, :].bitcast(I32), rows.bitcast(I32))
 
-        nc.sync.dma_start(tab_w[:, 0:TAB_CUT].bitcast(I32), tab_rows[:, 0:TAB_CUT])
         up_raw = sb([P, 2 * N], U8, "up_raw")
         nc.sync.dma_start(up_raw[:].bitcast(I32), upw_words[0].bitcast(I32))
+        nc.sync.dma_start(tab_w[:].bitcast(I32), tab_rows)
         move_scales(0)
-        nc.sync.dma_start(tab_w[:, TAB_CUT:T].bitcast(I32), tab_rows[:, TAB_CUT:T])
+        for u in range(2):
+            nc.sync.dma_start(dn_late[u][:], dn_rows[1][:, 2 * u : 2 * u + 2, :])
         wb_raw = sb([P, PASSES, N], U32, "wb_raw")
         nc.sync.dma_start(wb_raw[:].bitcast(I32), wb_words.rearrange("a p n i -> p a (n i)").bitcast(I32))
 
         x_rows = x0T.rearrange("(p t) c -> t p c", t=PACK)
         x_win = [sb([P, T], F32, "x_win%d" % t) for t in range(PACK)]
-        nc.sync.dma_start(x_win[0][:, 0:X_CUT], x_rows[0][:, 0:X_CUT])
         move_scales(1)
-        nc.sync.dma_start(x_win[0][:, X_CUT:T], x_rows[0][:, X_CUT:T])
-        for t in range(1, PACK):
+        for t in range(PACK):
             nc.sync.dma_start(x_win[t][:], x_rows[t])
 
         b_dealt = sb([P, P], F32, "b_dealt")
         nc.vector.tensor_scalar(
-            b_dealt[:].rearrange("p (t m) -> p t m", t=PACK), b_rows[:].rearrange("p (m t) -> p t m", t=PACK), 1.0, None, ALU.add
+            b_dealt[:].rearrange("p (t m) -> p t m", t=PACK),
+            b_rows[:].rearrange("p (m t) -> p t m", t=PACK),
+            1.0,
+            None,
+            ALU.add,
         )
         b_turned = sb([P, P], F32, "b_turned")
         nc.vector.transpose(b_turned[:], b_dealt[:])
-        b_low = at(AT_EARLY, [P, PACK - 1], F32, "b_low")
-        nc.vector.tensor_copy(b_low[:], b_turned[:, 0:96:32])
-        b_one = [b_low[:, t : t + 1] for t in range(PACK - 1)] + [b_turned[:, 96:97]]
+        last_slice = PACK - 1
+        b_low = shared.tile([P, last_slice], F32, name="b_low", align_bytes=64, offset=0)
+        nc.vector.tensor_copy(b_low[:], b_turned[:, 0 : last_slice * QUADRANT : QUADRANT])
+        b_one = [b_low[:, t : t + 1] for t in range(last_slice)]
+        b_one.append(b_turned[:, last_slice * QUADRANT : last_slice * QUADRANT + 1])
 
-        dn_w, dn_sc = [], []
-        for a in range(PASSES):
-            grouped = sb([P, PACK * R], BF16, "dn_grouped%d" % a)
+        def round_dn(grouped, raw, i0, copy=nc.scalar.copy):
             dealt = grouped[:].rearrange("p (t m i) -> p m i t", t=PACK, i=PACK)
-            rows = dn_raw[a][:].rearrange("p i (m t) -> p m i t", t=PACK)
-            nc.scalar.copy(dealt, rows)
+            rows = raw[:].rearrange("p i (m t) -> p m i t", t=PACK)
+            copy(dealt[:, :, i0 : i0 + raw.shape[1], :], rows)
+
+        def quantise_dn(a, grouped):
             codes = sb([P, R], U32, "dn_w%d" % a)
             scales = sb([P, R], U8, "dn_sc%d" % a)
             nc.vector.quantize_mx(out=codes[:].bitcast(FP8X4), scales=scales[:], in_=grouped[:])
             dn_w.append(codes)
             dn_sc.append(scales)
 
-        v_w = []
-        for h in range(halves):
-            both = sb([P, HALF], U32, "both%d" % h, tag="both")
+        def make_words(h, tag):
+            both = sb([P, HALF], U32, "both%d" % h, tag=tag)
             nc.vector.tensor_copy(both[:], listed(tab_w[:], h * HALF, (h + 1) * HALF))
             parted = sb([P, PASSES, 2 * HALF], U8, "parted%d" % h)
-            for cols in (slice(0, CHUNK), slice(CHUNK, HALF)) if h == 0 else (slice(0, HALF),):
-                nc.vector.tensor_copy(
-                    parted[:].bitcast(U16)[:, :, cols],
-                    both[:].bitcast(U16).rearrange("p (j a) -> p a j", a=PASSES)[:, :, cols],
-                )
+            nc.vector.tensor_copy(parted[:].bitcast(U16), both[:].bitcast(U16).rearrange("p (j a) -> p a j", a=PASSES))
             v_w.append(parted)
 
-        wb = sb([P, PASSES, N], U32, "wb")
+        dn_w, dn_sc, v_w = [], [], []
+        grouped0 = sb([P, PACK * R], BF16, "dn_grouped0")
+        round_dn(grouped0, dn_first, 0)
+        quantise_dn(0, grouped0)
+        grouped1 = sb([P, PACK * R], BF16, "dn_grouped1")
+        round_dn(grouped1, dn_late[0], 0)
+        make_words(0, None)
+        round_dn(grouped1, dn_late[1], 2, nc.vector.tensor_copy)
+        quantise_dn(1, grouped1)
+        make_words(1, "dn_grouped1")
+
+        wb = sb([P, PASSES, N], U32, "wb", tag="dn_grouped1")
         nc.vector.tensor_copy(
             wb[:].bitcast(I32).rearrange("p a (t m) -> p a m t", t=PACK),
             wb_raw[:].bitcast(I32).rearrange("p a (m t) -> p a m t", t=PACK),
@@ -158,120 +171,128 @@ def tile_list_xcross_reluP_kernel(
         )
 
         h_w, h_sc = [], []
-        for h in range(halves):
+        chunks = range(HALF // CHUNK)
+        for h in range(HALVES):
             h_bf = sb([P, HALF * PACK], BF16, "h_bf%d" % h)
-            for c in range(HALF // CHUNK):
-                bank = psum.tile([P, PACK, CHUNK], F32, name="hs%d_%d" % (h, c), tag="bank%d" % (4 + c))
+            banks = [
+                psum.tile([P, PACK, CHUNK], F32, name="hs%d_%d" % (h, c), tag="bank%d" % (HS_BANK + c)) for c in chunks
+            ]
+            if h == 0:
+                steps = [(c, a) for a in range(PASSES) for c in chunks]
+            else:
+                steps = [(c, a) for c in chunks for a in range(PASSES)]
+            for c, a in steps:
                 j0 = h * HALF + c * CHUNK
                 for t in range(PACK):
-                    for a in range(PASSES):
-                        nc.tensor.matmul_mx(
-                            out=bank[:, t, :],
-                            lhsT=dn_w[a][:, t * P : (t + 1) * P].bitcast(FP8X4),
-                            lhsT_scale=dn_sc[a][:, t * P : (t + 1) * P],
-                            rhs=v_w[h][:, a, 2 * c * CHUNK : 2 * (c + 1) * CHUNK].bitcast(FP4X4),
-                            rhs_scale=v_sc[a][:, j0 : j0 + CHUNK],
-                            start=(a == 0),
-                            stop=(a == PASSES - 1),
-                        )
-                nc.scalar.activation(
-                    h_bf[:, c * CHUNK * PACK : (c + 1) * CHUNK * PACK].rearrange("p (j t) -> p j t", t=PACK),
-                    bank[:].rearrange("p t j -> p j t"),
-                    ACT.Relu,
-                )
-            codes = sb([P, HALF], U32, "h_w%d" % h)
+                    nc.tensor.matmul_mx(
+                        out=banks[c][:, t, :],
+                        lhsT=dn_w[a][:, t * P : (t + 1) * P].bitcast(FP8X4),
+                        lhsT_scale=dn_sc[a][:, t * P : (t + 1) * P],
+                        rhs=v_w[h][:, a, 2 * c * CHUNK : 2 * (c + 1) * CHUNK].bitcast(FP4X4),
+                        rhs_scale=v_sc[a][:, j0 : j0 + CHUNK],
+                        start=(a == 0 and t == 0),
+                        stop=(a == PASSES - 1 and t == PACK - 1),
+                    )
+                if a == PASSES - 1:
+                    nc.scalar.activation(
+                        h_bf[:, c * CHUNK * PACK : (c + 1) * CHUNK * PACK].rearrange("p (j t) -> p j t", t=PACK),
+                        banks[c][:].rearrange("p t j -> p j t"),
+                        ACT.Relu,
+                    )
+            codes = sb([P, HALF], U32, "h_w%d" % h, tag="x_win0" if h == 1 else None)
             scales = sb([P, HALF], U8, "h_sc%d" % h)
             nc.vector.quantize_mx(out=codes[:].bitcast(FP8X4), scales=scales[:], in_=h_bf[:])
             h_w.append(codes)
             h_sc.append(scales)
             if h == 0:
                 x_first = sb([P, J], F32, "x_first", tag="h_bf0")
-                for part in range(halves):
+                for part in range(HALVES):
                     cols = slice(part * HALF, (part + 1) * HALF)
                     nc.vector.tensor_copy(x_first[:, cols], listed(x_win[0][:], cols.start, cols.stop))
 
-        o = sb([P, PACK, J], F32, "o")
-        z = {t: at(AT_LATE, [P, J], F32, "z2") if t == 2 else sb([P, J], F32, "z%d" % t) for t in range(1, PACK)}
-        for pair in range(2):
-            order = itertools.product(range(halves), (0, 1)) if pair == 0 else ((0, 2), (1, 2), (0, 3), (1, 3))
-            for turn, (h, t) in enumerate(order):
-                rows = slice(t * P, (t + 1) * P)
-                cols = slice(h * HALF, (h + 1) * HALF)
-                bank = psum.tile([P, HALF], F32, name="y%d_%d" % (t, h), tag="bank%d" % Y_BANKS[4 * pair + turn])
-                for a in range(PASSES):
-                    nc.tensor.matmul_mx(
-                        out=bank[:],
-                        lhsT=wb[:, a, rows].bitcast(FP8X4),
-                        lhsT_scale=plane1[:, J + a * N + rows.start : J + a * N + rows.stop],
-                        rhs=v_w[h][:, a, :].bitcast(FP4X4),
-                        rhs_scale=v_sc[a][:, cols],
-                        start=(a == 0),
-                        stop=False,
-                    )
+        o = sb([P, PACK, J], F32, "o", tag="h_bf1")
+        z = {t: sb([P, J], F32, "z%d" % t) for t in range(1, PACK)}
+
+        def cross(t, cols):
+            nc.vector.tensor_tensor(o[:, t, cols], listed(x_win[t][:], cols.start, cols.stop), z[t][:, cols], ALU.mult)
+
+        groups = [(t, h) for h in range(HALVES) for t in (0, 1)] + [(t, h) for t in (2, 3) for h in range(HALVES)]
+        for t, h in groups:
+            rows = slice(t * P, (t + 1) * P)
+            cols = slice(h * HALF, (h + 1) * HALF)
+            bank = psum.tile([P, HALF], F32, name="y%d_%d" % (t, h), tag="bank%d" % y_bank(t, h))
+            nc.tensor.matmul_mx(
+                out=bank[:],
+                lhsT=up[:, 2 * t * P : 2 * (t + 1) * P].bitcast(FP4X4),
+                lhsT_scale=plane1[:, J + PASSES * N + rows.start : J + PASSES * N + rows.stop],
+                rhs=h_w[h][:].bitcast(FP8X4),
+                rhs_scale=h_sc[h][:],
+                start=True,
+                stop=False,
+            )
+            for a in range(PASSES):
                 nc.tensor.matmul_mx(
                     out=bank[:],
-                    lhsT=up[:, 2 * t * P : 2 * (t + 1) * P].bitcast(FP4X4),
-                    lhsT_scale=plane1[:, J + PASSES * N + rows.start : J + PASSES * N + rows.stop],
-                    rhs=h_w[h][:].bitcast(FP8X4),
-                    rhs_scale=h_sc[h][:],
+                    lhsT=wb[:, a, rows].bitcast(FP8X4),
+                    lhsT_scale=plane1[:, J + a * N + rows.start : J + a * N + rows.stop],
+                    rhs=v_w[h][:, a, :].bitcast(FP4X4),
+                    rhs_scale=v_sc[a][:, cols],
                     start=False,
-                    stop=True,
+                    stop=(a == PASSES - 1),
                 )
-                if t == 0:
-                    nc.vector.scalar_tensor_tensor(
-                        o[:, 0, cols], bank[:], b_one[0], x_first[:, cols], ALU.add, ALU.mult
-                    )
-                else:
-                    nc.scalar.activation(z[t][:, cols], bank[:], ACT.Identity, bias=b_one[t])
-                if t == 1:
-                    nc.vector.tensor_tensor(o[:, 1, cols], listed(x_win[1][:], cols.start, cols.stop), z[1][:, cols], ALU.mult)
+            if t == 0:
+                nc.vector.scalar_tensor_tensor(o[:, 0, cols], bank[:], b_one[0], x_first[:, cols], ALU.add, ALU.mult)
+            else:
+                nc.scalar.activation(z[t][:, cols], bank[:], ACT.Identity, bias=b_one[t])
+            if t == 1:
+                cross(1, cols)
 
         out_rows = out_0.rearrange("(p t) j -> p t j", t=PACK)
         words_out = out_1[0].rearrange("p j i -> p (j i)").bitcast(I32)
         o_w = sb([P, J], U32, "o_w")
         o_sc = sb([P, J], U8, "o_sc")
-        cuts = [slice(EDGES[c], EDGES[c + 1]) for c in range(len(EDGES) - 1)]
-        o_early = at(AT_EARLY, [P, STORE_CUT, PACK], BF16, "o_early")
-        o_late = at(AT_LATE, [P, J - STORE_CUT, PACK], BF16, "o_late")
+        pieces = [slice(EDGES[c], EDGES[c + 1]) for c in range(len(EDGES) - 1)]
+        o_early = shared.tile([P, CUT, PACK], BF16, name="o_early", align_bytes=64, offset=0)
+        o_late = sb([P, J - CUT, PACK], BF16, "o_late")
         o_bf = [
-            o_early[:, cols, :] if cols.stop <= STORE_CUT else o_late[:, cols.start - STORE_CUT : cols.stop - STORE_CUT, :]
-            for cols in cuts
+            o_early[:, cols, :] if cols.stop <= CUT else o_late[:, cols.start - CUT : cols.stop - CUT, :]
+            for cols in pieces
         ]
+        early, late = slice(0, CUT), slice(CUT, J)
 
-        def cross(t, cols):
-            nc.vector.tensor_tensor(o[:, t, cols], listed(x_win[t][:], cols.start, cols.stop), z[t][:, cols], ALU.mult)
-
-        def round_pair(c, t0, copy=nc.scalar.copy):
-            copy(o_bf[c][:, :, t0 : t0 + 2], o[:, t0 : t0 + 2, cuts[c]].rearrange("p t j -> p j t"))
+        def round_upper(c, copy=nc.scalar.copy):
+            copy(o_bf[c][:, :, 2:4], o[:, 2:4, pieces[c]].rearrange("p t j -> p j t"))
 
         def quantise(c):
             nc.vector.quantize_mx(
-                out=o_w[:, cuts[c]].bitcast(FP8X4), scales=o_sc[:, cuts[c]], in_=o_bf[c].rearrange("p j t -> p (j t)")
+                out=o_w[:, pieces[c]].bitcast(FP8X4),
+                scales=o_sc[:, pieces[c]],
+                in_=o_bf[c].rearrange("p j t -> p (j t)"),
             )
 
         nc.sync.dma_start(out_rows[:, 0:2, :], o[:, 0:2, :])
-        nc.scalar.copy(o_early[:, :, 0:2], o[:, 0:2, 0:STORE_CUT].rearrange("p t j -> p j t"))
+        nc.scalar.copy(o_early[:, :, 0:2], o[:, 0:2, early].rearrange("p t j -> p j t"))
+        nc.vector.tensor_copy(o_late[:, :, 0:2], o[:, 0:2, late].rearrange("p t j -> p j t"))
         cross(2, slice(0, J))
-        nc.vector.tensor_copy(o_late[:, :, 0:2], o[:, 0:2, STORE_CUT:J].rearrange("p t j -> p j t"))
         nc.sync.dma_start(out_rows[:, 2, :], o[:, 2, :])
 
-        early, late = slice(0, STORE_CUT), slice(STORE_CUT, J)
-        last = len(cuts) - 1
+        last = len(pieces) - 1
         for c in range(last):
-            cross(3, cuts[c])
-            round_pair(c, 2)
-            if cuts[c].stop == STORE_CUT:
+            cross(3, pieces[c])
+            round_upper(c)
+            if pieces[c].stop == CUT:
                 nc.sync.dma_start(out_rows[:, 3, early], o[:, 3, early])
             if 0 < c < last - 1:
                 quantise(c - 1)
-        cross(3, cuts[last])
+        cross(3, pieces[last])
         nc.sync.dma_start(out_rows[:, 3, late], o[:, 3, late])
-        nc.sync.dma_start(words_out[:, 0:WORDS_CUT], o_w[:, 0:WORDS_CUT].bitcast(I32))
+        nc.sync.dma_start(words_out[:, early], o_w[:, early].bitcast(I32))
         quantise(last - 2)
-        round_pair(last, 2, nc.vector.tensor_copy)
+        round_upper(last, nc.vector.tensor_copy)
         quantise(last - 1)
         quantise(last)
-        nc.sync.dma_start(words_out[:, WORDS_CUT:J], o_w[:, WORDS_CUT:J].bitcast(I32))
-        for q in range(4):
+        nc.sync.dma_start(words_out[:, late], o_w[:, late].bitcast(I32))
+        for q in range(P // QUADRANT):
             queue = nc.sync if q < 2 else nc.scalar
-            queue.dma_start(out_2[0, 4 * q : 4 * q + 4, :].bitcast(I32), o_sc[32 * q : 32 * q + 4, :].bitcast(I32))
+            rows = o_sc[QUADRANT * q : QUADRANT * q + PACK, :]
+            queue.dma_start(out_2[0, PACK * q : PACK * (q + 1), :].bitcast(I32), rows.bitcast(I32))

@@ -27,6 +27,7 @@ LIST_ROWS = 16
 SPREAD = 4
 PASS_SPAN = 64
 HS_BANK = 4
+HS_BANKS = 3
 EDGES = (0, 128, 384, 640, 768, 896, 1024)
 CUT = 640
 
@@ -152,6 +153,11 @@ def tile_list_xcross_reluP_kernel(
         grouped0 = sb([P, PACK * R], BF16, "dn_grouped0")
         round_dn(grouped0, dn_first, 0)
         quantise_dn(0, grouped0)
+        up = sb([P, 2 * N], U8, "up")
+        nc.scalar.copy(
+            up[:].bitcast(U16).rearrange("p (t m) -> p m t", t=PACK),
+            up_raw[:].bitcast(U16).rearrange("p (m t) -> p m t", t=PACK),
+        )
         grouped1 = sb([P, PACK * R], BF16, "dn_grouped1")
         round_dn(grouped1, dn_late[0], 0)
         make_words(0, None)
@@ -164,25 +170,22 @@ def tile_list_xcross_reluP_kernel(
             wb[:].bitcast(I32).rearrange("p a (t m) -> p a m t", t=PACK),
             wb_raw[:].bitcast(I32).rearrange("p a (m t) -> p a m t", t=PACK),
         )
-        up = sb([P, 2 * N], U8, "up")
-        nc.vector.tensor_copy(
-            up[:].bitcast(U16).rearrange("p (t m) -> p m t", t=PACK),
-            up_raw[:].bitcast(U16).rearrange("p (m t) -> p m t", t=PACK),
-        )
 
         h_w, h_sc = [], []
         chunks = range(HALF // CHUNK)
         for h in range(HALVES):
             h_bf = sb([P, HALF * PACK], BF16, "h_bf%d" % h)
-            banks = [
-                psum.tile([P, PACK, CHUNK], F32, name="hs%d_%d" % (h, c), tag="bank%d" % (HS_BANK + c)) for c in chunks
-            ]
+            banks = {}
             if h == 0:
-                steps = [(c, a) for a in range(PASSES) for c in chunks]
+                steps = [(c, a) for a in range(PASSES) for c in range(HS_BANKS)]
+                steps += [(c, a) for c in range(HS_BANKS, len(chunks)) for a in range(PASSES)]
             else:
                 steps = [(c, a) for c in chunks for a in range(PASSES)]
             for c, a in steps:
                 j0 = h * HALF + c * CHUNK
+                if a == 0:
+                    tag = "bank%d" % (HS_BANK + j0 // CHUNK % HS_BANKS)
+                    banks[c] = psum.tile([P, PACK, CHUNK], F32, name="hs%d_%d" % (h, c), tag=tag)
                 for t in range(PACK):
                     nc.tensor.matmul_mx(
                         out=banks[c][:, t, :],

@@ -27,13 +27,11 @@ LIST_ROWS = 16
 SPREAD = 4
 PASS_SPAN = 64
 HS_BANK = 4
-HS_BANKS = 3
+HS_BANKS = 4
+EARLY_CUT = 640
+DN_CUT = 40
 EDGES = (0, 128, 384, 640, 768, 896, 1024)
 CUT = 640
-
-
-def y_bank(t, h):
-    return 2 * h + (0, 1, 1)[t] if t < PACK - 1 else 2 * (1 - h)
 
 
 def tile_list_xcross_reluP_kernel(
@@ -54,11 +52,7 @@ def tile_list_xcross_reluP_kernel(
 
         offsets = keep.tile([P, J // LIST_ROWS], U16, name="offsets")
 
-        dn_rows = dn.rearrange("(a p i) r -> a p i r", a=PASSES, i=PACK)
-        dn_first = sb([P, PACK, R], F32, "dn_raw0")
-        dn_late = [sb([P, 2, R], F32, "dn_late%d" % u) for u in range(2)]
-
-        tab_sc = sb([P, T], U8, "tab_sc")
+        tab_sc = shared.tile([P, T], U8, name="tab_sc", align_bytes=64, offset=6144)
         nc.vector.memset(tab_sc[:].bitcast(I32), 0)
         w_sc_raw = sb([P, PASSES + 1, N], U8, "w_sc_raw")
         nc.vector.memset(w_sc_raw[:].bitcast(I32), 0)
@@ -70,6 +64,13 @@ def tile_list_xcross_reluP_kernel(
         b_rows = sb([P, P], F32, "b_rows")
         nc.vector.memset(b_rows[:], 0.0)
 
+        wb_raw = shared.tile([P, PASSES, N], U32, name="wb_raw", align_bytes=64, offset=8192)
+        up_raw = sb([P, 2 * N], U8, "up_raw")
+        tab_w = sb([P, T], U32, "tab_w")
+        dn_rows = dn.rearrange("(a p i) r -> a p i r", a=PASSES, i=PACK)
+        dn_first = sb([P, PACK, R], F32, "dn_first")
+        dn_second = shared.tile([P, PACK, R], F32, name="dn_second", align_bytes=64, offset=0)
+
         nc.sync.dma_start(dn_first[:, 0:2, :], dn_rows[0][:, 0:2, :])
         nc.sync.dma_start(offsets[:], offs)
         nc.sync.dma_start(tab_sc[0:P:SPREAD, :].bitcast(I32), tab_scales.rearrange("a s t -> (a s) t").bitcast(I32))
@@ -78,9 +79,9 @@ def tile_list_xcross_reluP_kernel(
             w_sc_raw[PASS_SPAN:P:SPREAD, 0:PASSES, :].bitcast(I32), wb_scales.rearrange("a s n -> s a n").bitcast(I32)
         )
         nc.sync.dma_start(w_sc_raw[PASS_SPAN:P:SPREAD, PASSES, :].bitcast(I32), upw_scales[0].bitcast(I32))
+        nc.sync.dma_start(tab_w[:].bitcast(I32), tab_words[0].rearrange("p t i -> p (t i)").bitcast(I32))
+        nc.sync.dma_start(up_raw[:].bitcast(I32), upw_words[0].bitcast(I32))
         nc.sync.dma_start(b_rows[0:P:QUADRANT, :], b.rearrange("(q c) -> q c", c=P))
-        tab_w = sb([P, T], U32, "tab_w")
-        tab_rows = tab_words[0].rearrange("p t i -> p (t i)").bitcast(I32)
 
         g_sc = sb([P, J], U8, "g_sc")
         nc.vector.tensor_copy(g_sc[:], listed(tab_sc[:], 0, J))
@@ -99,18 +100,46 @@ def tile_list_xcross_reluP_kernel(
                 rows = source[first : first + (PACK - 1) * step + 1 : step, :]
                 nc.sync.dma_start(v_sc[a][r:P:QUADRANT, :].bitcast(I32), rows.bitcast(I32))
 
-        up_raw = sb([P, 2 * N], U8, "up_raw")
-        nc.sync.dma_start(up_raw[:].bitcast(I32), upw_words[0].bitcast(I32))
-        nc.sync.dma_start(tab_w[:].bitcast(I32), tab_rows)
         move_scales(0)
-        for u in range(2):
-            nc.sync.dma_start(dn_late[u][:], dn_rows[1][:, 2 * u : 2 * u + 2, :])
-        wb_raw = sb([P, PASSES, N], U32, "wb_raw")
+        nc.sync.dma_start(dn_second[:], dn_rows[1])
         nc.sync.dma_start(wb_raw[:].bitcast(I32), wb_words.rearrange("a p n i -> p a (n i)").bitcast(I32))
-
-        x_rows = x0T.rearrange("(p t) c -> t p c", t=PACK)
-        x_win = [sb([P, T], F32, "x_win%d" % t) for t in range(PACK)]
         move_scales(1)
+        up = sb([P, 2 * N], U8, "up")
+        dn_w, dn_sc, v_w = [], [], []
+        grouped = [sb([P, PACK * R], BF16, "dn_grouped%d" % a) for a in range(PASSES)]
+
+        dealt = [g[:].rearrange("p (t m i) -> p m i t", t=PACK, i=PACK) for g in grouped]
+
+        def by_column(raw):
+            return raw[:].rearrange("p i (m t) -> p m i t", t=PACK)
+
+        def quantise_dn(a):
+            codes = sb([P, R], U32, "dn_w%d" % a)
+            scales = sb([P, R], U8, "dn_sc%d" % a)
+            nc.vector.quantize_mx(out=codes[:].bitcast(FP8X4), scales=scales[:], in_=grouped[a][:])
+            dn_w.append(codes)
+            dn_sc.append(scales)
+
+        def gather_words(h, tag):
+            both = sb([P, HALF], U32, "both%d" % h, tag=tag)
+            nc.vector.tensor_copy(both[:], listed(tab_w[:], h * HALF, (h + 1) * HALF))
+            return both
+
+        def part_words(h, both):
+            parted = sb([P, PASSES, 2 * HALF], U8, "parted%d" % h)
+            nc.vector.tensor_copy(parted[:].bitcast(U16), both[:].bitcast(U16).rearrange("p (j a) -> p a j", a=PASSES))
+            v_w.append(parted)
+
+        for u in range(2):
+            nc.scalar.copy(dealt[0][:, :, 2 * u : 2 * u + 2, :], by_column(dn_first)[:, :, 2 * u : 2 * u + 2, :])
+        quantise_dn(0)
+        nc.scalar.copy(
+            up[:].bitcast(U16).rearrange("p (t m) -> p m t", t=PACK),
+            up_raw[:].bitcast(U16).rearrange("p (m t) -> p m t", t=PACK),
+        )
+        x_rows = x0T.rearrange("(p t) c -> t p c", t=PACK)
+        x_tags = ("dn_first", "up_raw", "w_sc_raw", "staged")
+        x_win = [sb([P, T], F32, "x_win%d" % t, tag=x_tags[t]) for t in range(PACK)]
         for t in range(PACK):
             nc.sync.dma_start(x_win[t][:], x_rows[t])
 
@@ -124,94 +153,95 @@ def tile_list_xcross_reluP_kernel(
         )
         b_turned = sb([P, P], F32, "b_turned")
         nc.vector.transpose(b_turned[:], b_dealt[:])
-        last_slice = PACK - 1
-        b_low = shared.tile([P, last_slice], F32, name="b_low", align_bytes=64, offset=0)
-        nc.vector.tensor_copy(b_low[:], b_turned[:, 0 : last_slice * QUADRANT : QUADRANT])
-        b_one = [b_low[:, t : t + 1] for t in range(last_slice)]
-        b_one.append(b_turned[:, last_slice * QUADRANT : last_slice * QUADRANT + 1])
+        b_one = [b_turned[:, t * QUADRANT : t * QUADRANT + 1] for t in range(PACK)]
 
-        def round_dn(grouped, raw, i0, copy=nc.scalar.copy):
-            dealt = grouped[:].rearrange("p (t m i) -> p m i t", t=PACK, i=PACK)
-            rows = raw[:].rearrange("p i (m t) -> p m i t", t=PACK)
-            copy(dealt[:, :, i0 : i0 + raw.shape[1], :], rows)
-
-        def quantise_dn(a, grouped):
-            codes = sb([P, R], U32, "dn_w%d" % a)
-            scales = sb([P, R], U8, "dn_sc%d" % a)
-            nc.vector.quantize_mx(out=codes[:].bitcast(FP8X4), scales=scales[:], in_=grouped[:])
-            dn_w.append(codes)
-            dn_sc.append(scales)
-
-        def make_words(h, tag):
-            both = sb([P, HALF], U32, "both%d" % h, tag=tag)
-            nc.vector.tensor_copy(both[:], listed(tab_w[:], h * HALF, (h + 1) * HALF))
-            parted = sb([P, PASSES, 2 * HALF], U8, "parted%d" % h)
-            nc.vector.tensor_copy(parted[:].bitcast(U16), both[:].bitcast(U16).rearrange("p (j a) -> p a j", a=PASSES))
-            v_w.append(parted)
-
-        dn_w, dn_sc, v_w = [], [], []
-        grouped0 = sb([P, PACK * R], BF16, "dn_grouped0")
-        round_dn(grouped0, dn_first, 0)
-        quantise_dn(0, grouped0)
-        up = sb([P, 2 * N], U8, "up")
+        part_words(0, gather_words(0, None))
+        nc.scalar.copy(dealt[1][:, 0:DN_CUT], by_column(dn_second)[:, 0:DN_CUT])
+        nc.vector.tensor_copy(dealt[1][:, DN_CUT:P], by_column(dn_second)[:, DN_CUT:P])
+        quantise_dn(1)
+        part_words(1, gather_words(1, "dn_grouped1"))
+        wb = sb([P, PASSES, N], U32, "wb")
         nc.scalar.copy(
-            up[:].bitcast(U16).rearrange("p (t m) -> p m t", t=PACK),
-            up_raw[:].bitcast(U16).rearrange("p (m t) -> p m t", t=PACK),
-        )
-        grouped1 = sb([P, PACK * R], BF16, "dn_grouped1")
-        round_dn(grouped1, dn_late[0], 0)
-        make_words(0, None)
-        round_dn(grouped1, dn_late[1], 2, nc.vector.tensor_copy)
-        quantise_dn(1, grouped1)
-        make_words(1, "dn_grouped1")
-
-        wb = sb([P, PASSES, N], U32, "wb", tag="dn_grouped1")
-        nc.vector.tensor_copy(
-            wb[:].bitcast(I32).rearrange("p a (t m) -> p a m t", t=PACK),
-            wb_raw[:].bitcast(I32).rearrange("p a (m t) -> p a m t", t=PACK),
+            wb[:].rearrange("p a (t m) -> p a m t", t=PACK), wb_raw[:].rearrange("p a (m t) -> p a m t", t=PACK)
         )
 
-        h_w, h_sc = [], []
-        chunks = range(HALF // CHUNK)
-        for h in range(HALVES):
-            h_bf = sb([P, HALF * PACK], BF16, "h_bf%d" % h)
-            banks = {}
-            if h == 0:
-                steps = [(c, a) for a in range(PASSES) for c in range(HS_BANKS)]
-                steps += [(c, a) for c in range(HS_BANKS, len(chunks)) for a in range(PASSES)]
-            else:
-                steps = [(c, a) for c in chunks for a in range(PASSES)]
-            for c, a in steps:
-                j0 = h * HALF + c * CHUNK
-                if a == 0:
-                    tag = "bank%d" % (HS_BANK + j0 // CHUNK % HS_BANKS)
-                    banks[c] = psum.tile([P, PACK, CHUNK], F32, name="hs%d_%d" % (h, c), tag=tag)
-                for t in range(PACK):
-                    nc.tensor.matmul_mx(
-                        out=banks[c][:, t, :],
-                        lhsT=dn_w[a][:, t * P : (t + 1) * P].bitcast(FP8X4),
-                        lhsT_scale=dn_sc[a][:, t * P : (t + 1) * P],
-                        rhs=v_w[h][:, a, 2 * c * CHUNK : 2 * (c + 1) * CHUNK].bitcast(FP4X4),
-                        rhs_scale=v_sc[a][:, j0 : j0 + CHUNK],
-                        start=(a == 0 and t == 0),
-                        stop=(a == PASSES - 1 and t == PACK - 1),
-                    )
-                if a == PASSES - 1:
-                    nc.scalar.activation(
-                        h_bf[:, c * CHUNK * PACK : (c + 1) * CHUNK * PACK].rearrange("p (j t) -> p j t", t=PACK),
-                        banks[c][:].rearrange("p t j -> p j t"),
-                        ACT.Relu,
-                    )
-            codes = sb([P, HALF], U32, "h_w%d" % h, tag="x_win0" if h == 1 else None)
+        y = {}
+
+        def open_y(t, h, bank):
+            y[t, h] = psum.tile([P, HALF], F32, name="y%d_%d" % (t, h), tag="bank%d" % bank)
+
+        def wb_pass(t, h, a):
+            first = J + a * N + t * P
+            nc.tensor.matmul_mx(
+                out=y[t, h][:],
+                lhsT=wb[:, a, t * P : (t + 1) * P].bitcast(FP8X4),
+                lhsT_scale=plane1[:, first : first + P],
+                rhs=v_w[h][:, a, :].bitcast(FP4X4),
+                rhs_scale=v_sc[a][:, h * HALF : (h + 1) * HALF],
+                start=(a == 0),
+                stop=False,
+            )
+
+        def up_pass(t, h):
+            first = J + PASSES * N + t * P
+            nc.tensor.matmul_mx(
+                out=y[t, h][:],
+                lhsT=up[:, 2 * t * P : 2 * (t + 1) * P].bitcast(FP4X4),
+                lhsT_scale=plane1[:, first : first + P],
+                rhs=h_w[h][:].bitcast(FP8X4),
+                rhs_scale=h_sc[h][:],
+                start=False,
+                stop=True,
+            )
+
+        hs = {}
+
+        def hs_pass(c, a):
+            h, j0 = c * CHUNK // HALF, c * CHUNK
+            if a == 0:
+                hs[c] = psum.tile([P, PACK, CHUNK], F32, name="hs%d" % c, tag="bank%d" % (HS_BANK + c % HS_BANKS))
+            for t in range(PACK):
+                nc.tensor.matmul_mx(
+                    out=hs[c][:, t, :],
+                    lhsT=dn_w[a][:, t * P : (t + 1) * P].bitcast(FP8X4),
+                    lhsT_scale=dn_sc[a][:, t * P : (t + 1) * P],
+                    rhs=v_w[h][:, a, 2 * (j0 - h * HALF) : 2 * (j0 - h * HALF + CHUNK)].bitcast(FP4X4),
+                    rhs_scale=v_sc[a][:, j0 : j0 + CHUNK],
+                    start=(a == 0 and t == 0),
+                    stop=(a == PASSES - 1 and t == PACK - 1),
+                )
+
+        def relu(c):
+            h, j0 = c * CHUNK // HALF, c * CHUNK % HALF
+            side_by_side = h_bf[h][:, j0 * PACK : (j0 + CHUNK) * PACK].rearrange("p (j t) -> p j t", t=PACK)
+            sums = hs[c][:].rearrange("p t j -> p j t")
+            nc.scalar.activation(side_by_side, sums, ACT.Relu)
+
+        def quantise_h(h, tag):
+            codes = sb([P, HALF], U32, "h_w%d" % h, tag=tag)
             scales = sb([P, HALF], U8, "h_sc%d" % h)
-            nc.vector.quantize_mx(out=codes[:].bitcast(FP8X4), scales=scales[:], in_=h_bf[:])
+            nc.vector.quantize_mx(out=codes[:].bitcast(FP8X4), scales=scales[:], in_=h_bf[h][:])
             h_w.append(codes)
             h_sc.append(scales)
-            if h == 0:
-                x_first = sb([P, J], F32, "x_first", tag="h_bf0")
-                for part in range(HALVES):
-                    cols = slice(part * HALF, (part + 1) * HALF)
-                    nc.vector.tensor_copy(x_first[:, cols], listed(x_win[0][:], cols.start, cols.stop))
+
+        h_bf = [sb([P, HALF * PACK], BF16, "h_bf%d" % h) for h in range(HALVES)]
+        h_w, h_sc = [], []
+        per_half = HALF // CHUNK
+        low = [(t, h) for h in range(HALVES) for t in (0, 1)]
+        high = [(t, h) for t in (2, 3) for h in range(HALVES)]
+        for c in range(per_half):
+            hs_pass(c, 0)
+        for c in range(per_half):
+            hs_pass(c, 1)
+            relu(c)
+        quantise_h(0, None)
+        x_first = sb([P, J], F32, "x_first", tag="h_bf0")
+        nc.vector.tensor_copy(x_first[:], listed(x_win[0][:], 0, J))
+        for c in range(per_half, 2 * per_half):
+            for a in range(PASSES):
+                hs_pass(c, a)
+            relu(c)
+        quantise_h(1, "dn_first")
 
         o = sb([P, PACK, J], F32, "o", tag="h_bf1")
         z = {t: sb([P, J], F32, "z%d" % t) for t in range(1, PACK)}
@@ -219,81 +249,59 @@ def tile_list_xcross_reluP_kernel(
         def cross(t, cols):
             nc.vector.tensor_tensor(o[:, t, cols], listed(x_win[t][:], cols.start, cols.stop), z[t][:, cols], ALU.mult)
 
-        groups = [(t, h) for h in range(HALVES) for t in (0, 1)] + [(t, h) for t in (2, 3) for h in range(HALVES)]
-        for t, h in groups:
-            rows = slice(t * P, (t + 1) * P)
+        def leave(t, h):
             cols = slice(h * HALF, (h + 1) * HALF)
-            bank = psum.tile([P, HALF], F32, name="y%d_%d" % (t, h), tag="bank%d" % y_bank(t, h))
-            nc.tensor.matmul_mx(
-                out=bank[:],
-                lhsT=up[:, 2 * t * P : 2 * (t + 1) * P].bitcast(FP4X4),
-                lhsT_scale=plane1[:, J + PASSES * N + rows.start : J + PASSES * N + rows.stop],
-                rhs=h_w[h][:].bitcast(FP8X4),
-                rhs_scale=h_sc[h][:],
-                start=True,
-                stop=False,
-            )
-            for a in range(PASSES):
-                nc.tensor.matmul_mx(
-                    out=bank[:],
-                    lhsT=wb[:, a, rows].bitcast(FP8X4),
-                    lhsT_scale=plane1[:, J + a * N + rows.start : J + a * N + rows.stop],
-                    rhs=v_w[h][:, a, :].bitcast(FP4X4),
-                    rhs_scale=v_sc[a][:, cols],
-                    start=False,
-                    stop=(a == PASSES - 1),
-                )
             if t == 0:
-                nc.vector.scalar_tensor_tensor(o[:, 0, cols], bank[:], b_one[0], x_first[:, cols], ALU.add, ALU.mult)
+                nc.vector.scalar_tensor_tensor(o[:, 0, cols], y[t, h][:], b_one[0], x_first[:, cols], ALU.add, ALU.mult)
             else:
-                nc.scalar.activation(z[t][:, cols], bank[:], ACT.Identity, bias=b_one[t])
-            if t == 1:
-                cross(1, cols)
+                nc.scalar.activation(z[t][:, cols], y[t, h][:], ACT.Identity, bias=b_one[t])
+
+        for bank, (t, h) in enumerate(low + high):
+            open_y(t, h, bank % 4)
+            for a in range(PASSES):
+                wb_pass(t, h, a)
+            up_pass(t, h)
+            leave(t, h)
+            if (t, h) == low[-1]:
+                cross(1, slice(0, J))
 
         out_rows = out_0.rearrange("(p t) j -> p t j", t=PACK)
         words_out = out_1[0].rearrange("p j i -> p (j i)").bitcast(I32)
         o_w = sb([P, J], U32, "o_w")
         o_sc = sb([P, J], U8, "o_sc")
+        o_bf = sb([P, J, PACK], BF16, "o_bf")
         pieces = [slice(EDGES[c], EDGES[c + 1]) for c in range(len(EDGES) - 1)]
-        o_early = shared.tile([P, CUT, PACK], BF16, name="o_early", align_bytes=64, offset=0)
-        o_late = sb([P, J - CUT, PACK], BF16, "o_late")
-        o_bf = [
-            o_early[:, cols, :] if cols.stop <= CUT else o_late[:, cols.start - CUT : cols.stop - CUT, :]
-            for cols in pieces
-        ]
-        early, late = slice(0, CUT), slice(CUT, J)
 
-        def round_upper(c, copy=nc.scalar.copy):
-            copy(o_bf[c][:, :, 2:4], o[:, 2:4, pieces[c]].rearrange("p t j -> p j t"))
+        def round_pair(u, cols, copy):
+            copy(o_bf[:, cols, 2 * u : 2 * u + 2], o[:, 2 * u : 2 * u + 2, cols].rearrange("p t j -> p j t"))
 
-        def quantise(c):
+        def quantise(cols):
             nc.vector.quantize_mx(
-                out=o_w[:, pieces[c]].bitcast(FP8X4),
-                scales=o_sc[:, pieces[c]],
-                in_=o_bf[c].rearrange("p j t -> p (j t)"),
+                out=o_w[:, cols].bitcast(FP8X4), scales=o_sc[:, cols], in_=o_bf[:, cols, :].rearrange("p j t -> p (j t)")
             )
 
         nc.sync.dma_start(out_rows[:, 0:2, :], o[:, 0:2, :])
-        nc.scalar.copy(o_early[:, :, 0:2], o[:, 0:2, early].rearrange("p t j -> p j t"))
-        nc.vector.tensor_copy(o_late[:, :, 0:2], o[:, 0:2, late].rearrange("p t j -> p j t"))
+        round_pair(0, slice(0, EARLY_CUT), nc.scalar.copy)
+        round_pair(0, slice(EARLY_CUT, J), nc.vector.tensor_copy)
         cross(2, slice(0, J))
         nc.sync.dma_start(out_rows[:, 2, :], o[:, 2, :])
 
+        early, late = slice(0, CUT), slice(CUT, J)
         last = len(pieces) - 1
         for c in range(last):
             cross(3, pieces[c])
-            round_upper(c)
+            round_pair(1, pieces[c], nc.scalar.copy)
             if pieces[c].stop == CUT:
                 nc.sync.dma_start(out_rows[:, 3, early], o[:, 3, early])
             if 0 < c < last - 1:
-                quantise(c - 1)
+                quantise(pieces[c - 1])
         cross(3, pieces[last])
         nc.sync.dma_start(out_rows[:, 3, late], o[:, 3, late])
         nc.sync.dma_start(words_out[:, early], o_w[:, early].bitcast(I32))
-        quantise(last - 2)
-        round_upper(last, nc.vector.tensor_copy)
-        quantise(last - 1)
-        quantise(last)
+        quantise(pieces[last - 2])
+        round_pair(1, pieces[last], nc.vector.tensor_copy)
+        quantise(pieces[last - 1])
+        quantise(pieces[last])
         nc.sync.dma_start(words_out[:, late], o_w[:, late].bitcast(I32))
         for q in range(P // QUADRANT):
             queue = nc.sync if q < 2 else nc.scalar

@@ -41,7 +41,6 @@ def tile_list_xcross_reluP_kernel(
 
     with ExitStack() as ctx:
         keep = ctx.enter_context(tc.tile_pool(name="keep", bufs=1))
-        shared = ctx.enter_context(tc.tile_pool(name="shared", bufs=1))
         psum = ctx.enter_context(tc.psum_pool(name="psum", bufs=1))
 
         def sb(shape, dtype, name, tag=None):
@@ -52,7 +51,7 @@ def tile_list_xcross_reluP_kernel(
 
         offsets = keep.tile([P, J // LIST_ROWS], U16, name="offsets")
 
-        tab_sc = shared.tile([P, T], U8, name="tab_sc", align_bytes=64, offset=6144)
+        tab_sc = sb([P, T], U8, "tab_sc")
         nc.vector.memset(tab_sc[:].bitcast(I32), 0)
         w_sc_raw = sb([P, PASSES + 1, N], U8, "w_sc_raw")
         nc.vector.memset(w_sc_raw[:].bitcast(I32), 0)
@@ -64,17 +63,17 @@ def tile_list_xcross_reluP_kernel(
         b_rows = sb([P, P], F32, "b_rows")
         nc.vector.memset(b_rows[:], 0.0)
 
-        wb_raw = shared.tile([P, PASSES, N], U32, name="wb_raw", align_bytes=64, offset=8192)
+        wb_raw = sb([P, PASSES, N], U32, "wb_raw")
         up_raw = sb([P, 2 * N], U8, "up_raw")
         tab_w = sb([P, T], U32, "tab_w")
         dn_rows = dn.rearrange("(a p i) r -> a p i r", a=PASSES, i=PACK)
         dn_first = sb([P, PACK, R], F32, "dn_first")
-        dn_second = shared.tile([P, PACK, R], F32, name="dn_second", align_bytes=64, offset=0)
+        dn_second = sb([P, PACK, R], F32, "dn_second")
 
-        nc.sync.dma_start(dn_first[:, 0:2, :], dn_rows[0][:, 0:2, :])
+        nc.sync.dma_start(wb_raw[:].bitcast(I32), wb_words.rearrange("a p n i -> p a (n i)").bitcast(I32))
         nc.sync.dma_start(offsets[:], offs)
         nc.sync.dma_start(tab_sc[0:P:SPREAD, :].bitcast(I32), tab_scales.rearrange("a s t -> (a s) t").bitcast(I32))
-        nc.sync.dma_start(dn_first[:, 2:4, :], dn_rows[0][:, 2:4, :])
+        nc.sync.dma_start(dn_first[:], dn_rows[0])
         nc.sync.dma_start(
             w_sc_raw[PASS_SPAN:P:SPREAD, 0:PASSES, :].bitcast(I32), wb_scales.rearrange("a s n -> s a n").bitcast(I32)
         )
@@ -102,7 +101,6 @@ def tile_list_xcross_reluP_kernel(
 
         move_scales(0)
         nc.sync.dma_start(dn_second[:], dn_rows[1])
-        nc.sync.dma_start(wb_raw[:].bitcast(I32), wb_words.rearrange("a p n i -> p a (n i)").bitcast(I32))
         move_scales(1)
         up = sb([P, 2 * N], U8, "up")
         dn_w, dn_sc, v_w = [], [], []
@@ -130,16 +128,18 @@ def tile_list_xcross_reluP_kernel(
             nc.vector.tensor_copy(parted[:].bitcast(U16), both[:].bitcast(U16).rearrange("p (j a) -> p a j", a=PASSES))
             v_w.append(parted)
 
-        for u in range(2):
-            nc.scalar.copy(dealt[0][:, :, 2 * u : 2 * u + 2, :], by_column(dn_first)[:, :, 2 * u : 2 * u + 2, :])
+        wb = sb([P, PASSES, N], U32, "wb")
+        nc.scalar.copy(
+            wb[:].rearrange("p a (t m) -> p a m t", t=PACK), wb_raw[:].rearrange("p a (m t) -> p a m t", t=PACK)
+        )
+        nc.scalar.copy(dealt[0], by_column(dn_first))
         quantise_dn(0)
         nc.scalar.copy(
             up[:].bitcast(U16).rearrange("p (t m) -> p m t", t=PACK),
             up_raw[:].bitcast(U16).rearrange("p (m t) -> p m t", t=PACK),
         )
         x_rows = x0T.rearrange("(p t) c -> t p c", t=PACK)
-        x_tags = ("dn_first", "up_raw", "w_sc_raw", "staged")
-        x_win = [sb([P, T], F32, "x_win%d" % t, tag=x_tags[t]) for t in range(PACK)]
+        x_win = [sb([P, T], F32, "x_win%d" % t) for t in range(PACK)]
         for t in range(PACK):
             nc.sync.dma_start(x_win[t][:], x_rows[t])
 
@@ -160,10 +160,6 @@ def tile_list_xcross_reluP_kernel(
         nc.vector.tensor_copy(dealt[1][:, DN_CUT:P], by_column(dn_second)[:, DN_CUT:P])
         quantise_dn(1)
         part_words(1, gather_words(1, "dn_grouped1"))
-        wb = sb([P, PASSES, N], U32, "wb")
-        nc.scalar.copy(
-            wb[:].rearrange("p a (t m) -> p a m t", t=PACK), wb_raw[:].rearrange("p a (m t) -> p a m t", t=PACK)
-        )
 
         y = {}
 
@@ -241,7 +237,7 @@ def tile_list_xcross_reluP_kernel(
             for a in range(PASSES):
                 hs_pass(c, a)
             relu(c)
-        quantise_h(1, "dn_first")
+        quantise_h(1, "x_win0")
 
         o = sb([P, PACK, J], F32, "o", tag="h_bf1")
         z = {t: sb([P, J], F32, "z%d" % t) for t in range(1, PACK)}

@@ -44,12 +44,12 @@ def tile_list_xcross_reluP_kernel(
         psum = ctx.enter_context(tc.psum_pool(name="psum", bufs=1))
 
         def sb(shape, dtype, name, tag=None):
-            return keep.tile(shape, dtype, name=name, tag=tag or name, align_bytes=64)
+            return keep.tile(shape, dtype, name=name, tag=tag or name, align_bytes=256)
 
         def listed(window, j0, j1):
             return window.indirect(offsets[:, j0 // LIST_ROWS : j1 // LIST_ROWS])
 
-        offsets = keep.tile([P, J // LIST_ROWS], U16, name="offsets")
+        offsets = keep.tile([P, J // LIST_ROWS], U16, name="offsets", align_bytes=256)
 
         tab_sc = sb([P, T], U8, "tab_sc")
         nc.vector.memset(tab_sc[:].bitcast(I32), 0)

@@ -299,7 +299,7 @@ def tile_list_xcross_reluP_kernel(
         quantise(pieces[last - 1])
         quantise(pieces[last])
         nc.sync.dma_start(words_out[:, late], o_w[:, late].bitcast(I32))
-        for q in range(P // QUADRANT):
-            queue = nc.sync if q < 2 else nc.scalar
-            rows = o_sc[QUADRANT * q : QUADRANT * q + PACK, :]
-            queue.dma_start(out_2[0, PACK * q : PACK * (q + 1), :].bitcast(I32), rows.bitcast(I32))
+        scale_rows = out_2[0].rearrange("(q r) j -> r q j", r=PACK).bitcast(I32)
+        for r in range(PACK):
+            queue = nc.sync if r < 2 else nc.scalar
+            queue.dma_start(scale_rows[r], o_sc[r:P:QUADRANT, :].bitcast(I32))

@@ -26,10 +26,13 @@ CHUNK = 128
 LIST_ROWS = 16
 SPREAD = 4
 PASS_SPAN = 64
+WEIGHT_PLANES = PASSES + 1
+PLANE_BYTES = PASSES * J + WEIGHT_PLANES * N
 HS_BANK = 4
 HS_BANKS = 4
-EARLY_CUT = 640
-DN_CUT = 40
+EARLY_CUT = 768
+DN_CUT = 80
+PIECE = 256
 EDGES = (0, 128, 384, 640, 768, 896, 1024)
 CUT = 640
 
@@ -53,63 +56,57 @@ def tile_list_xcross_reluP_kernel(
 
         tab_sc = sb([P, T], U8, "tab_sc")
         nc.vector.memset(tab_sc[:].bitcast(I32), 0)
-        w_sc_raw = sb([P, PASSES + 1, N], U8, "w_sc_raw")
+        w_sc_raw = sb([P, WEIGHT_PLANES, N], U8, "w_sc_raw")
         nc.vector.memset(w_sc_raw[:].bitcast(I32), 0)
-        plane0 = sb([P, J], U8, "plane0")
-        nc.vector.memset(plane0[:].bitcast(I32), 0)
-        plane1 = sb([P, J + (PASSES + 1) * N], U8, "plane1")
-        nc.vector.memset(plane1[:].bitcast(I32), 0)
-        v_sc = [plane0, plane1]
         b_rows = sb([P, P], F32, "b_rows")
         nc.vector.memset(b_rows[:], 0.0)
+        planes = sb([P, PLANE_BYTES], U8, "planes")
+        nc.vector.memset(planes[:].bitcast(I32), 0)
 
         wb_raw = sb([P, PASSES, N], U32, "wb_raw")
         up_raw = sb([P, 2 * N], U8, "up_raw")
         tab_w = sb([P, T], U32, "tab_w")
         dn_rows = dn.rearrange("(a p i) r -> a p i r", a=PASSES, i=PACK)
-        dn_first = sb([P, PACK, R], F32, "dn_first")
-        dn_second = sb([P, PACK, R], F32, "dn_second")
+        dn_raw = [sb([P, PACK, R], F32, "dn_raw%d" % a) for a in range(PASSES)]
 
         nc.sync.dma_start(wb_raw[:].bitcast(I32), wb_words.rearrange("a p n i -> p a (n i)").bitcast(I32))
         nc.sync.dma_start(offsets[:], offs)
         nc.sync.dma_start(tab_sc[0:P:SPREAD, :].bitcast(I32), tab_scales.rearrange("a s t -> (a s) t").bitcast(I32))
-        nc.sync.dma_start(dn_first[:], dn_rows[0])
-        nc.sync.dma_start(
-            w_sc_raw[PASS_SPAN:P:SPREAD, 0:PASSES, :].bitcast(I32), wb_scales.rearrange("a s n -> s a n").bitcast(I32)
-        )
-        nc.sync.dma_start(w_sc_raw[PASS_SPAN:P:SPREAD, PASSES, :].bitcast(I32), upw_scales[0].bitcast(I32))
+        nc.sync.dma_start(dn_raw[0][:], dn_rows[0])
+        w_rows = w_sc_raw[0:PASS_SPAN:SPREAD]
+        nc.sync.dma_start(w_rows[:, 0:PASSES, :].bitcast(I32), wb_scales.rearrange("a s n -> s a n").bitcast(I32))
+        nc.sync.dma_start(w_rows[:, PASSES, :].bitcast(I32), upw_scales[0].bitcast(I32))
+        nc.sync.dma_start(b_rows[0:P:QUADRANT, :], b.rearrange("(q c) -> q c", c=P))
+        nc.sync.dma_start(dn_raw[1][:], dn_rows[1])
         nc.sync.dma_start(tab_w[:].bitcast(I32), tab_words[0].rearrange("p t i -> p (t i)").bitcast(I32))
         nc.sync.dma_start(up_raw[:].bitcast(I32), upw_words[0].bitcast(I32))
-        nc.sync.dma_start(b_rows[0:P:QUADRANT, :], b.rearrange("(q c) -> q c", c=P))
 
         g_sc = sb([P, J], U8, "g_sc")
         nc.vector.tensor_copy(g_sc[:], listed(tab_sc[:], 0, J))
-        staged = sb([P, J + (PASSES + 1) * N], U8, "staged")
-        nc.vector.tensor_copy(staged[:, 0:J].bitcast(I32), g_sc[:].bitcast(I32))
+        staged = sb([P, PLANE_BYTES], U8, "staged")
+        for a in range(PASSES):
+            nc.vector.tensor_copy(
+                staged[0:PASS_SPAN, a * J : (a + 1) * J].bitcast(I32),
+                g_sc[a * PASS_SPAN : (a + 1) * PASS_SPAN, :].bitcast(I32),
+            )
         nc.vector.tensor_copy(
-            staged[:, J:].rearrange("p (a t m) -> p a m t", a=PASSES + 1, t=PACK),
+            staged[:, PASSES * J :].rearrange("p (a t m) -> p a m t", a=WEIGHT_PLANES, t=PACK),
             w_sc_raw[:].rearrange("p a (m t) -> p a m t", t=PACK),
         )
+        for r in range(PACK):
+            rows = staged[SPREAD * r : PASS_SPAN : PACK * SPREAD, :]
+            nc.sync.dma_start(planes[r:P:QUADRANT, :].bitcast(I32), rows.bitcast(I32))
 
-        def move_scales(a):
-            source = (g_sc, staged)[a]
-            step = PACK * SPREAD
-            for r in range(PACK):
-                first = PASS_SPAN * a + SPREAD * r
-                rows = source[first : first + (PACK - 1) * step + 1 : step, :]
-                nc.sync.dma_start(v_sc[a][r:P:QUADRANT, :].bitcast(I32), rows.bitcast(I32))
+        x_rows = x0T.rearrange("(p t) c -> t p c", t=PACK)
+        x_win = [sb([P, T], F32, "x_win%d" % t) for t in range(PACK)]
+        for t in range(PACK):
+            nc.sync.dma_start(x_win[t][:], x_rows[t])
 
-        move_scales(0)
-        nc.sync.dma_start(dn_second[:], dn_rows[1])
-        move_scales(1)
-        up = sb([P, 2 * N], U8, "up")
-        dn_w, dn_sc, v_w = [], [], []
+        dn_w, dn_sc = [], []
+        v_w = [sb([P, PASSES, 2 * HALF], U8, "parted%d" % h) for h in range(HALVES)]
         grouped = [sb([P, PACK * R], BF16, "dn_grouped%d" % a) for a in range(PASSES)]
-
         dealt = [g[:].rearrange("p (t m i) -> p m i t", t=PACK, i=PACK) for g in grouped]
-
-        def by_column(raw):
-            return raw[:].rearrange("p i (m t) -> p m i t", t=PACK)
+        by_column = [raw[:].rearrange("p i (m t) -> p m i t", t=PACK) for raw in dn_raw]
 
         def quantise_dn(a):
             codes = sb([P, R], U32, "dn_w%d" % a)
@@ -118,30 +115,19 @@ def tile_list_xcross_reluP_kernel(
             dn_w.append(codes)
             dn_sc.append(scales)
 
-        def gather_words(h, tag):
-            both = sb([P, HALF], U32, "both%d" % h, tag=tag)
-            nc.vector.tensor_copy(both[:], listed(tab_w[:], h * HALF, (h + 1) * HALF))
-            return both
-
-        def part_words(h, both):
-            parted = sb([P, PASSES, 2 * HALF], U8, "parted%d" % h)
-            nc.vector.tensor_copy(parted[:].bitcast(U16), both[:].bitcast(U16).rearrange("p (j a) -> p a j", a=PASSES))
-            v_w.append(parted)
+        def gather_words(g):
+            both = sb([P, PIECE], U32, "both%d" % g, tag="both%d" % (g % 2))
+            nc.vector.tensor_copy(both[:], listed(tab_w[:], g * PIECE, (g + 1) * PIECE))
+            j0 = g * PIECE % HALF
+            parted = v_w[g * PIECE // HALF][:, :, 2 * j0 : 2 * (j0 + PIECE)]
+            nc.vector.tensor_copy(parted.bitcast(U16), both[:].bitcast(U16).rearrange("p (j a) -> p a j", a=PASSES))
 
         wb = sb([P, PASSES, N], U32, "wb")
         nc.scalar.copy(
             wb[:].rearrange("p a (t m) -> p a m t", t=PACK), wb_raw[:].rearrange("p a (m t) -> p a m t", t=PACK)
         )
-        nc.scalar.copy(dealt[0], by_column(dn_first))
+        nc.scalar.copy(dealt[0], by_column[0])
         quantise_dn(0)
-        nc.scalar.copy(
-            up[:].bitcast(U16).rearrange("p (t m) -> p m t", t=PACK),
-            up_raw[:].bitcast(U16).rearrange("p (m t) -> p m t", t=PACK),
-        )
-        x_rows = x0T.rearrange("(p t) c -> t p c", t=PACK)
-        x_win = [sb([P, T], F32, "x_win%d" % t) for t in range(PACK)]
-        for t in range(PACK):
-            nc.sync.dma_start(x_win[t][:], x_rows[t])
 
         b_dealt = sb([P, P], F32, "b_dealt")
         nc.vector.tensor_scalar(
@@ -155,11 +141,27 @@ def tile_list_xcross_reluP_kernel(
         nc.vector.transpose(b_turned[:], b_dealt[:])
         b_one = [b_turned[:, t * QUADRANT : t * QUADRANT + 1] for t in range(PACK)]
 
-        part_words(0, gather_words(0, None))
-        nc.scalar.copy(dealt[1][:, 0:DN_CUT], by_column(dn_second)[:, 0:DN_CUT])
-        nc.vector.tensor_copy(dealt[1][:, DN_CUT:P], by_column(dn_second)[:, DN_CUT:P])
+        nc.scalar.copy(dealt[1][:, 0:DN_CUT], by_column[1][:, 0:DN_CUT])
+        nc.vector.tensor_copy(dealt[1][:, DN_CUT:P], by_column[1][:, DN_CUT:P])
         quantise_dn(1)
-        part_words(1, gather_words(1, "dn_grouped1"))
+        up = sb([P, 2 * N], U8, "up")
+        nc.scalar.copy(
+            up[:].bitcast(U16).rearrange("p (t m) -> p m t", t=PACK),
+            up_raw[:].bitcast(U16).rearrange("p (m t) -> p m t", t=PACK),
+        )
+        for g in range(J // PIECE):
+            gather_words(g)
+
+        def table_words(a, j0, j1):
+            h = j0 // HALF
+            return v_w[h][:, a, 2 * (j0 - h * HALF) : 2 * (j1 - h * HALF)].bitcast(FP4X4)
+
+        def table_scales(a, j0, j1):
+            return planes[:, a * J + j0 : a * J + j1]
+
+        def weight_scales(plane, t):
+            first = PASSES * J + plane * N + t * P
+            return planes[:, first : first + P]
 
         y = {}
 
@@ -167,23 +169,21 @@ def tile_list_xcross_reluP_kernel(
             y[t, h] = psum.tile([P, HALF], F32, name="y%d_%d" % (t, h), tag="bank%d" % bank)
 
         def wb_pass(t, h, a):
-            first = J + a * N + t * P
             nc.tensor.matmul_mx(
                 out=y[t, h][:],
                 lhsT=wb[:, a, t * P : (t + 1) * P].bitcast(FP8X4),
-                lhsT_scale=plane1[:, first : first + P],
-                rhs=v_w[h][:, a, :].bitcast(FP4X4),
-                rhs_scale=v_sc[a][:, h * HALF : (h + 1) * HALF],
+                lhsT_scale=weight_scales(a, t),
+                rhs=table_words(a, h * HALF, (h + 1) * HALF),
+                rhs_scale=table_scales(a, h * HALF, (h + 1) * HALF),
                 start=(a == 0),
                 stop=False,
             )
 
         def up_pass(t, h):
-            first = J + PASSES * N + t * P
             nc.tensor.matmul_mx(
                 out=y[t, h][:],
                 lhsT=up[:, 2 * t * P : 2 * (t + 1) * P].bitcast(FP4X4),
-                lhsT_scale=plane1[:, first : first + P],
+                lhsT_scale=weight_scales(PASSES, t),
                 rhs=h_w[h][:].bitcast(FP8X4),
                 rhs_scale=h_sc[h][:],
                 start=False,
@@ -193,7 +193,7 @@ def tile_list_xcross_reluP_kernel(
         hs = {}
 
         def hs_pass(c, a):
-            h, j0 = c * CHUNK // HALF, c * CHUNK
+            j0 = c * CHUNK
             if a == 0:
                 hs[c] = psum.tile([P, PACK, CHUNK], F32, name="hs%d" % c, tag="bank%d" % (HS_BANK + c % HS_BANKS))
             for t in range(PACK):
@@ -201,8 +201,8 @@ def tile_list_xcross_reluP_kernel(
                     out=hs[c][:, t, :],
                     lhsT=dn_w[a][:, t * P : (t + 1) * P].bitcast(FP8X4),
                     lhsT_scale=dn_sc[a][:, t * P : (t + 1) * P],
-                    rhs=v_w[h][:, a, 2 * (j0 - h * HALF) : 2 * (j0 - h * HALF + CHUNK)].bitcast(FP4X4),
-                    rhs_scale=v_sc[a][:, j0 : j0 + CHUNK],
+                    rhs=table_words(a, j0, j0 + CHUNK),
+                    rhs_scale=table_scales(a, j0, j0 + CHUNK),
                     start=(a == 0 and t == 0),
                     stop=(a == PASSES - 1 and t == PACK - 1),
                 )
@@ -223,53 +223,60 @@ def tile_list_xcross_reluP_kernel(
         h_bf = [sb([P, HALF * PACK], BF16, "h_bf%d" % h) for h in range(HALVES)]
         h_w, h_sc = [], []
         per_half = HALF // CHUNK
-        low = [(t, h) for h in range(HALVES) for t in (0, 1)]
-        high = [(t, h) for t in (2, 3) for h in range(HALVES)]
         for c in range(per_half):
-            hs_pass(c, 0)
-        for c in range(per_half):
-            hs_pass(c, 1)
+            for a in range(PASSES):
+                hs_pass(c, a)
             relu(c)
-        quantise_h(0, None)
-        x_first = sb([P, J], F32, "x_first", tag="h_bf0")
+        x_first = sb([P, J], F32, "x_first")
         nc.vector.tensor_copy(x_first[:], listed(x_win[0][:], 0, J))
+        quantise_h(0, "x_win0")
         for c in range(per_half, 2 * per_half):
             for a in range(PASSES):
                 hs_pass(c, a)
             relu(c)
-        quantise_h(1, "x_win0")
+        quantise_h(1, "h_bf0")
 
         o = sb([P, PACK, J], F32, "o", tag="h_bf1")
-        z = {t: sb([P, J], F32, "z%d" % t) for t in range(1, PACK)}
+        o_bf = sb([P, J, PACK], BF16, "o_bf")
+        z = {}
+
+        def round_pair(u, cols, copy):
+            copy(o_bf[:, cols, 2 * u : 2 * u + 2], o[:, 2 * u : 2 * u + 2, cols].rearrange("p t j -> p j t"))
 
         def cross(t, cols):
             nc.vector.tensor_tensor(o[:, t, cols], listed(x_win[t][:], cols.start, cols.stop), z[t][:, cols], ALU.mult)
 
-        def leave(t, h):
+        def make_y(t, h, bank):
             cols = slice(h * HALF, (h + 1) * HALF)
+            open_y(t, h, bank)
+            for a in range(PASSES):
+                wb_pass(t, h, a)
+            up_pass(t, h)
             if t == 0:
                 nc.vector.scalar_tensor_tensor(o[:, 0, cols], y[t, h][:], b_one[0], x_first[:, cols], ALU.add, ALU.mult)
             else:
                 nc.scalar.activation(z[t][:, cols], y[t, h][:], ACT.Identity, bias=b_one[t])
 
-        for bank, (t, h) in enumerate(low + high):
-            open_y(t, h, bank % 4)
-            for a in range(PASSES):
-                wb_pass(t, h, a)
-            up_pass(t, h)
-            leave(t, h)
-            if (t, h) == low[-1]:
-                cross(1, slice(0, J))
+        z[1] = sb([P, J], F32, "z1")
+        for h in range(HALVES):
+            make_y(0, h, 2 * h)
+            make_y(1, h, 2 * h + 1)
+            cross(1, slice(h * HALF, (h + 1) * HALF))
+        z[2] = sb([P, J], F32, "z2")
+        for h in range(HALVES):
+            make_y(2, h, h)
+        round_pair(0, slice(0, HALF), nc.scalar.copy)
+        round_pair(0, slice(HALF, EARLY_CUT), nc.scalar.copy)
+        round_pair(0, slice(EARLY_CUT, J), nc.vector.tensor_copy)
+        z[3] = sb([P, J], F32, "z3", tag="z1")
+        for h in range(HALVES):
+            make_y(3, h, 2 + h)
 
         out_rows = out_0.rearrange("(p t) j -> p t j", t=PACK)
         words_out = out_1[0].rearrange("p j i -> p (j i)").bitcast(I32)
         o_w = sb([P, J], U32, "o_w")
         o_sc = sb([P, J], U8, "o_sc")
-        o_bf = sb([P, J, PACK], BF16, "o_bf")
         pieces = [slice(EDGES[c], EDGES[c + 1]) for c in range(len(EDGES) - 1)]
-
-        def round_pair(u, cols, copy):
-            copy(o_bf[:, cols, 2 * u : 2 * u + 2], o[:, 2 * u : 2 * u + 2, cols].rearrange("p t j -> p j t"))
 
         def quantise(cols):
             nc.vector.quantize_mx(
@@ -277,8 +284,6 @@ def tile_list_xcross_reluP_kernel(
             )
 
         nc.sync.dma_start(out_rows[:, 0:2, :], o[:, 0:2, :])
-        round_pair(0, slice(0, EARLY_CUT), nc.scalar.copy)
-        round_pair(0, slice(EARLY_CUT, J), nc.vector.tensor_copy)
         cross(2, slice(0, J))
         nc.sync.dma_start(out_rows[:, 2, :], o[:, 2, :])
 

@@ -30,11 +30,12 @@ WEIGHT_PLANES = PASSES + 1
 PLANE_BYTES = PASSES * J + WEIGHT_PLANES * N
 HS_BANK = 4
 HS_BANKS = 4
-EARLY_CUT = 768
+EARLY_CUT = 640
 DN_CUT = 80
-PIECE = 256
+PIECE = 512
 EDGES = (0, 128, 384, 640, 768, 896, 1024)
 CUT = 640
+GATHER_EDGES = (0, 128, 384, 640, 896)
 
 
 def tile_list_xcross_reluP_kernel(
@@ -71,10 +72,13 @@ def tile_list_xcross_reluP_kernel(
 
         nc.sync.dma_start(wb_raw[:].bitcast(I32), wb_words.rearrange("a p n i -> p a (n i)").bitcast(I32))
         nc.sync.dma_start(offsets[:], offs)
-        nc.sync.dma_start(tab_sc[0:P:SPREAD, :].bitcast(I32), tab_scales.rearrange("a s t -> (a s) t").bitcast(I32))
+        for a in range(PASSES):
+            spread = tab_sc[a * PASS_SPAN : (a + 1) * PASS_SPAN : SPREAD, :]
+            nc.sync.dma_start(spread.bitcast(I32), tab_scales[a].bitcast(I32))
         nc.sync.dma_start(dn_raw[0][:], dn_rows[0])
         w_rows = w_sc_raw[0:PASS_SPAN:SPREAD]
-        nc.sync.dma_start(w_rows[:, 0:PASSES, :].bitcast(I32), wb_scales.rearrange("a s n -> s a n").bitcast(I32))
+        for a in range(PASSES):
+            nc.sync.dma_start(w_rows[:, a, :].bitcast(I32), wb_scales[a].bitcast(I32))
         nc.sync.dma_start(w_rows[:, PASSES, :].bitcast(I32), upw_scales[0].bitcast(I32))
         nc.sync.dma_start(b_rows[0:P:QUADRANT, :], b.rearrange("(q c) -> q c", c=P))
         nc.sync.dma_start(dn_raw[1][:], dn_rows[1])
@@ -116,7 +120,7 @@ def tile_list_xcross_reluP_kernel(
             dn_sc.append(scales)
 
         def gather_words(g):
-            both = sb([P, PIECE], U32, "both%d" % g, tag="both%d" % (g % 2))
+            both = sb([P, PIECE], U32, "both%d" % g, tag="both")
             nc.vector.tensor_copy(both[:], listed(tab_w[:], g * PIECE, (g + 1) * PIECE))
             j0 = g * PIECE % HALF
             parted = v_w[g * PIECE // HALF][:, :, 2 * j0 : 2 * (j0 + PIECE)]
@@ -130,12 +134,11 @@ def tile_list_xcross_reluP_kernel(
         quantise_dn(0)
 
         b_dealt = sb([P, P], F32, "b_dealt")
-        nc.vector.tensor_scalar(
+        nc.scalar.activation(
             b_dealt[:].rearrange("p (t m) -> p t m", t=PACK),
             b_rows[:].rearrange("p (m t) -> p t m", t=PACK),
-            1.0,
-            None,
-            ALU.add,
+            ACT.Identity,
+            bias=1.0,
         )
         b_turned = sb([P, P], F32, "b_turned")
         nc.vector.transpose(b_turned[:], b_dealt[:])
@@ -289,8 +292,10 @@ def tile_list_xcross_reluP_kernel(
 
         early, late = slice(0, CUT), slice(CUT, J)
         last = len(pieces) - 1
+        gathers = {j0: slice(j0, j1) for j0, j1 in zip(GATHER_EDGES, GATHER_EDGES[1:])}
         for c in range(last):
-            cross(3, pieces[c])
+            if pieces[c].start in gathers:
+                cross(3, gathers[pieces[c].start])
             round_pair(1, pieces[c], nc.scalar.copy)
             if pieces[c].stop == CUT:
                 nc.sync.dma_start(out_rows[:, 3, early], o[:, 3, early])

@@ -281,6 +281,9 @@ def tile_list_xcross_reluP_kernel(
         o_sc = sb([P, J], U8, "o_sc")
         pieces = [slice(EDGES[c], EDGES[c + 1]) for c in range(len(EDGES) - 1)]
 
+        def store_codes(j0, j1):
+            nc.sync.dma_start(words_out[:, j0:j1], o_w[:, j0:j1].bitcast(I32))
+
         def quantise(cols):
             nc.vector.quantize_mx(
                 out=o_w[:, cols].bitcast(FP8X4), scales=o_sc[:, cols], in_=o_bf[:, cols, :].rearrange("p j t -> p (j t)")
@@ -303,13 +306,13 @@ def tile_list_xcross_reluP_kernel(
                 quantise(pieces[c - 1])
         cross(3, pieces[last])
         nc.sync.dma_start(out_rows[:, 3, late], o[:, 3, late])
-        nc.sync.dma_start(words_out[:, early], o_w[:, early].bitcast(I32))
+        store_codes(0, 384)
         quantise(pieces[last - 2])
+        store_codes(384, 768)
         round_pair(1, pieces[last], nc.vector.tensor_copy)
         quantise(pieces[last - 1])
         quantise(pieces[last])
-        nc.sync.dma_start(words_out[:, late], o_w[:, late].bitcast(I32))
+        store_codes(768, J)
         scale_rows = out_2[0].rearrange("(q r) j -> r q j", r=PACK).bitcast(I32)
         for r in range(PACK):
-            queue = nc.sync if r < 2 else nc.scalar
-            queue.dma_start(scale_rows[r], o_sc[r:P:QUADRANT, :].bitcast(I32))
+            nc.sync.dma_start(scale_rows[r], o_sc[r:P:QUADRANT, :].bitcast(I32))

from contextlib import ExitStack

import concourse.mybir as mybir

K, R, N, T, J = 1024, 512, 512, 4096, 1024
FLOPS = 2 * J * (K * R + K * N + R * N)

F32 = mybir.dt.float32
BF16 = mybir.dt.bfloat16
I32 = mybir.dt.int32
U32 = mybir.dt.uint32
U16 = mybir.dt.uint16
U8 = mybir.dt.uint8
FP8X4 = mybir.dt.float8_e4m3fn_x4
FP4X4 = mybir.dt.float4_e2m1fn_x4
ACT = mybir.ActivationFunctionType
ALU = mybir.AluOpType

P = 128
PACK = 4
QUADRANT = 32
PASSES = K // (P * PACK)
HALF = 512
HALVES = J // HALF
CHUNK = 128
LIST_ROWS = 16
SPREAD = 4
PASS_SPAN = 64
WEIGHT_PLANES = PASSES + 1
PLANE_BYTES = PASSES * J + WEIGHT_PLANES * N
HS_BANK = 4
HS_BANKS = 4
EARLY_CUT = 640
DN_CUT = 80
PIECE = 512
EDGES = (0, 128, 384, 640, 768, 896, 1024)
CUT = 640
GATHER_EDGES = (0, 128, 384, 640, 896)


def tile_list_xcross_reluP_kernel(
    tc, tab_words, tab_scales, wb_words, wb_scales, dn, upw_words, upw_scales, x0T, b, offs, out_0, out_1, out_2
):
    nc = tc.nc

    with ExitStack() as ctx:
        keep = ctx.enter_context(tc.tile_pool(name="keep", bufs=1))
        psum = ctx.enter_context(tc.psum_pool(name="psum", bufs=1))

        def sb(shape, dtype, name, tag=None):
            return keep.tile(shape, dtype, name=name, tag=tag or name, align_bytes=256)

        def listed(window, j0, j1):
            return window.indirect(offsets[:, j0 // LIST_ROWS : j1 // LIST_ROWS])

        offsets = keep.tile([P, J // LIST_ROWS], U16, name="offsets", align_bytes=256)

        tab_sc = sb([P, T], U8, "tab_sc")
        nc.vector.memset(tab_sc[:].bitcast(I32), 0)
        w_sc_raw = sb([P, WEIGHT_PLANES, N], U8, "w_sc_raw")
        nc.vector.memset(w_sc_raw[:].bitcast(I32), 0)
        b_rows = sb([P, P], F32, "b_rows")
        nc.vector.memset(b_rows[:], 0.0)
        planes = sb([P, PLANE_BYTES], U8, "planes")
        nc.vector.memset(planes[:].bitcast(I32), 0)

        wb_raw = sb([P, PASSES, N], U32, "wb_raw")
        up_raw = sb([P, 2 * N], U8, "up_raw")
        tab_w = sb([P, T], U32, "tab_w")
        dn_rows = dn.rearrange("(a p i) r -> a p i r", a=PASSES, i=PACK)
        dn_raw = [sb([P, PACK, R], F32, "dn_raw%d" % a) for a in range(PASSES)]

        nc.sync.dma_start(wb_raw[:].bitcast(I32), wb_words.rearrange("a p n i -> p a (n i)").bitcast(I32))
        nc.sync.dma_start(offsets[:], offs)
        for a in range(PASSES):
            spread = tab_sc[a * PASS_SPAN : (a + 1) * PASS_SPAN : SPREAD, :]
            nc.sync.dma_start(spread.bitcast(I32), tab_scales[a].bitcast(I32))
        nc.sync.dma_start(dn_raw[0][:], dn_rows[0])
        w_rows = w_sc_raw[0:PASS_SPAN:SPREAD]
        for a in range(PASSES):
            nc.sync.dma_start(w_rows[:, a, :].bitcast(I32), wb_scales[a].bitcast(I32))
        nc.sync.dma_start(w_rows[:, PASSES, :].bitcast(I32), upw_scales[0].bitcast(I32))
        nc.sync.dma_start(b_rows[0:P:QUADRANT, :], b.rearrange("(q c) -> q c", c=P))
        nc.sync.dma_start(dn_raw[1][:], dn_rows[1])
        nc.sync.dma_start(tab_w[:].bitcast(I32), tab_words[0].rearrange("p t i -> p (t i)").bitcast(I32))
        nc.sync.dma_start(up_raw[:].bitcast(I32), upw_words[0].bitcast(I32))

        g_sc = sb([P, J], U8, "g_sc")
        nc.vector.tensor_copy(g_sc[:], listed(tab_sc[:], 0, J))
        staged = sb([P, PLANE_BYTES], U8, "staged")
        for a in range(PASSES):
            nc.vector.tensor_copy(
                staged[0:PASS_SPAN, a * J : (a + 1) * J].bitcast(I32),
                g_sc[a * PASS_SPAN : (a + 1) * PASS_SPAN, :].bitcast(I32),
            )
        nc.vector.tensor_copy(
            staged[:, PASSES * J :].rearrange("p (a t m) -> p a m t", a=WEIGHT_PLANES, t=PACK),
            w_sc_raw[:].rearrange("p a (m t) -> p a m t", t=PACK),
        )
        for r in range(PACK):
            rows = staged[SPREAD * r : PASS_SPAN : PACK * SPREAD, :]
            nc.sync.dma_start(planes[r:P:QUADRANT, :].bitcast(I32), rows.bitcast(I32))

        x_rows = x0T.rearrange("(p t) c -> t p c", t=PACK)
        x_win = [sb([P, T], F32, "x_win%d" % t) for t in range(PACK)]
        for t in range(PACK):
            nc.sync.dma_start(x_win[t][:], x_rows[t])

        dn_w, dn_sc = [], []
        v_w = [sb([P, PASSES, 2 * HALF], U8, "parted%d" % h) for h in range(HALVES)]
        grouped = [sb([P, PACK * R], BF16, "dn_grouped%d" % a) for a in range(PASSES)]
        dealt = [g[:].rearrange("p (t m i) -> p m i t", t=PACK, i=PACK) for g in grouped]
        by_column = [raw[:].rearrange("p i (m t) -> p m i t", t=PACK) for raw in dn_raw]

        def quantise_dn(a):
            codes = sb([P, R], U32, "dn_w%d" % a)
            scales = sb([P, R], U8, "dn_sc%d" % a)
            nc.vector.quantize_mx(out=codes[:].bitcast(FP8X4), scales=scales[:], in_=grouped[a][:])
            dn_w.append(codes)
            dn_sc.append(scales)

        def gather_words(g):
            both = sb([P, PIECE], U32, "both%d" % g, tag="both")
            nc.vector.tensor_copy(both[:], listed(tab_w[:], g * PIECE, (g + 1) * PIECE))
            j0 = g * PIECE % HALF
            parted = v_w[g * PIECE // HALF][:, :, 2 * j0 : 2 * (j0 + PIECE)]
            nc.vector.tensor_copy(parted.bitcast(U16), both[:].bitcast(U16).rearrange("p (j a) -> p a j", a=PASSES))

        wb = sb([P, PASSES, N], U32, "wb")
        nc.scalar.copy(
            wb[:].rearrange("p a (t m) -> p a m t", t=PACK), wb_raw[:].rearrange("p a (m t) -> p a m t", t=PACK)
        )
        nc.scalar.copy(dealt[0], by_column[0])
        quantise_dn(0)

        b_dealt = sb([P, P], F32, "b_dealt")
        nc.scalar.activation(
            b_dealt[:].rearrange("p (t m) -> p t m", t=PACK),
            b_rows[:].rearrange("p (m t) -> p t m", t=PACK),
            ACT.Identity,
            bias=1.0,
        )
        b_turned = sb([P, P], F32, "b_turned")
        nc.vector.transpose(b_turned[:], b_dealt[:])
        b_one = [b_turned[:, t * QUADRANT : t * QUADRANT + 1] for t in range(PACK)]

        nc.scalar.copy(dealt[1][:, 0:DN_CUT], by_column[1][:, 0:DN_CUT])
        nc.vector.tensor_copy(dealt[1][:, DN_CUT:P], by_column[1][:, DN_CUT:P])
        quantise_dn(1)
        up = sb([P, 2 * N], U8, "up")
        nc.scalar.copy(
            up[:].bitcast(U16).rearrange("p (t m) -> p m t", t=PACK),
            up_raw[:].bitcast(U16).rearrange("p (m t) -> p m t", t=PACK),
        )
        for g in range(J // PIECE):
            gather_words(g)

        def table_words(a, j0, j1):
            h = j0 // HALF
            return v_w[h][:, a, 2 * (j0 - h * HALF) : 2 * (j1 - h * HALF)].bitcast(FP4X4)

        def table_scales(a, j0, j1):
            return planes[:, a * J + j0 : a * J + j1]

        def weight_scales(plane, t):
            first = PASSES * J + plane * N + t * P
            return planes[:, first : first + P]

        y = {}

        def open_y(t, h, bank):
            y[t, h] = psum.tile([P, HALF], F32, name="y%d_%d" % (t, h), tag="bank%d" % bank)

        def wb_pass(t, h, a):
            nc.tensor.matmul_mx(
                out=y[t, h][:],
                lhsT=wb[:, a, t * P : (t + 1) * P].bitcast(FP8X4),
                lhsT_scale=weight_scales(a, t),
                rhs=table_words(a, h * HALF, (h + 1) * HALF),
                rhs_scale=table_scales(a, h * HALF, (h + 1) * HALF),
                start=(a == 0),
                stop=False,
            )

        def up_pass(t, h):
            nc.tensor.matmul_mx(
                out=y[t, h][:],
                lhsT=up[:, 2 * t * P : 2 * (t + 1) * P].bitcast(FP4X4),
                lhsT_scale=weight_scales(PASSES, t),
                rhs=h_w[h][:].bitcast(FP8X4),
                rhs_scale=h_sc[h][:],
                start=False,
                stop=True,
            )

        hs = {}

        def hs_pass(c, a):
            j0 = c * CHUNK
            if a == 0:
                hs[c] = psum.tile([P, PACK, CHUNK], F32, name="hs%d" % c, tag="bank%d" % (HS_BANK + c % HS_BANKS))
            for t in range(PACK):
                nc.tensor.matmul_mx(
                    out=hs[c][:, t, :],
                    lhsT=dn_w[a][:, t * P : (t + 1) * P].bitcast(FP8X4),
                    lhsT_scale=dn_sc[a][:, t * P : (t + 1) * P],
                    rhs=table_words(a, j0, j0 + CHUNK),
                    rhs_scale=table_scales(a, j0, j0 + CHUNK),
                    start=(a == 0 and t == 0),
                    stop=(a == PASSES - 1 and t == PACK - 1),
                )

        def relu(c):
            h, j0 = c * CHUNK // HALF, c * CHUNK % HALF
            side_by_side = h_bf[h][:, j0 * PACK : (j0 + CHUNK) * PACK].rearrange("p (j t) -> p j t", t=PACK)
            sums = hs[c][:].rearrange("p t j -> p j t")
            nc.scalar.activation(side_by_side, sums, ACT.Relu)

        def quantise_h(h, tag):
            codes = sb([P, HALF], U32, "h_w%d" % h, tag=tag)
            scales = sb([P, HALF], U8, "h_sc%d" % h)
            nc.vector.quantize_mx(out=codes[:].bitcast(FP8X4), scales=scales[:], in_=h_bf[h][:])
            h_w.append(codes)
            h_sc.append(scales)

        h_bf = [sb([P, HALF * PACK], BF16, "h_bf%d" % h) for h in range(HALVES)]
        h_w, h_sc = [], []
        per_half = HALF // CHUNK
        for c in range(per_half):
            for a in range(PASSES):
                hs_pass(c, a)
            relu(c)
        x_first = sb([P, J], F32, "x_first")
        nc.vector.tensor_copy(x_first[:], listed(x_win[0][:], 0, J))
        quantise_h(0, "x_win0")
        for c in range(per_half, 2 * per_half):
            for a in range(PASSES):
                hs_pass(c, a)
            relu(c)
        quantise_h(1, "h_bf0")

        o = sb([P, PACK, J], F32, "o", tag="h_bf1")
        o_bf = sb([P, J, PACK], BF16, "o_bf")
        z = {}

        def round_pair(u, cols, copy):
            copy(o_bf[:, cols, 2 * u : 2 * u + 2], o[:, 2 * u : 2 * u + 2, cols].rearrange("p t j -> p j t"))

        def cross(t, cols):
            nc.vector.tensor_tensor(o[:, t, cols], listed(x_win[t][:], cols.start, cols.stop), z[t][:, cols], ALU.mult)

        def make_y(t, h, bank):
            cols = slice(h * HALF, (h + 1) * HALF)
            open_y(t, h, bank)
            for a in range(PASSES):
                wb_pass(t, h, a)
            up_pass(t, h)
            if t == 0:
                nc.vector.scalar_tensor_tensor(o[:, 0, cols], y[t, h][:], b_one[0], x_first[:, cols], ALU.add, ALU.mult)
            else:
                nc.scalar.activation(z[t][:, cols], y[t, h][:], ACT.Identity, bias=b_one[t])

        z[1] = sb([P, J], F32, "z1")
        for h in range(HALVES):
            make_y(0, h, 2 * h)
            make_y(1, h, 2 * h + 1)
            cross(1, slice(h * HALF, (h + 1) * HALF))
        z[2] = sb([P, J], F32, "z2")
        for h in range(HALVES):
            make_y(2, h, h)
        round_pair(0, slice(0, HALF), nc.scalar.copy)
        round_pair(0, slice(HALF, EARLY_CUT), nc.scalar.copy)
        round_pair(0, slice(EARLY_CUT, J), nc.vector.tensor_copy)
        z[3] = sb([P, J], F32, "z3", tag="z1")
        for h in range(HALVES):
            make_y(3, h, 2 + h)

        out_rows = out_0.rearrange("(p t) j -> p t j", t=PACK)
        words_out = out_1[0].rearrange("p j i -> p (j i)").bitcast(I32)
        o_w = sb([P, J], U32, "o_w")
        o_sc = sb([P, J], U8, "o_sc")
        pieces = [slice(EDGES[c], EDGES[c + 1]) for c in range(len(EDGES) - 1)]

        def store_codes(j0, j1):
            nc.sync.dma_start(words_out[:, j0:j1], o_w[:, j0:j1].bitcast(I32))

        def quantise(cols):
            nc.vector.quantize_mx(
                out=o_w[:, cols].bitcast(FP8X4), scales=o_sc[:, cols], in_=o_bf[:, cols, :].rearrange("p j t -> p (j t)")
            )

        nc.sync.dma_start(out_rows[:, 0:2, :], o[:, 0:2, :])
        cross(2, slice(0, J))
        nc.sync.dma_start(out_rows[:, 2, :], o[:, 2, :])

        early, late = slice(0, CUT), slice(CUT, J)
        last = len(pieces) - 1
        gathers = {j0: slice(j0, j1) for j0, j1 in zip(GATHER_EDGES, GATHER_EDGES[1:])}
        for c in range(last):
            if pieces[c].start in gathers:
                cross(3, gathers[pieces[c].start])
            round_pair(1, pieces[c], nc.scalar.copy)
            if pieces[c].stop == CUT:
                nc.sync.dma_start(out_rows[:, 3, early], o[:, 3, early])
            if 0 < c < last - 1:
                quantise(pieces[c - 1])
        cross(3, pieces[last])
        nc.sync.dma_start(out_rows[:, 3, late], o[:, 3, late])
        store_codes(0, 384)
        quantise(pieces[last - 2])
        store_codes(384, 768)
        round_pair(1, pieces[last], nc.vector.tensor_copy)
        quantise(pieces[last - 1])
        quantise(pieces[last])
        store_codes(768, J)
        scale_rows = out_2[0].rearrange("(q r) j -> r q j", r=PACK).bitcast(I32)
        for r in range(PACK):
            nc.sync.dma_start(scale_rows[r], o_sc[r:P:QUADRANT, :].bitcast(I32))
